import numpy as np
import ml_dtypes


def mxq(x, axis, fmt="e4m3"):
    dtype, down = {"e4m3": (ml_dtypes.float8_e4m3fn, 7), "e5m2": (ml_dtypes.float8_e5m2, 14)}[fmt]
    v = np.moveaxis(np.asarray(x, np.float32).astype(ml_dtypes.bfloat16).astype(np.float64), axis, -1)
    blocks = v.reshape(v.shape[:-1] + (-1, 32))
    amax = np.abs(blocks).max(-1, keepdims=True)
    byte = np.maximum(np.where(amax > 0, np.frexp(amax)[1] - 1 + 127, 0) - down, 1)
    scale = np.exp2(byte - 127.0)
    codes = (blocks / scale).astype(np.float32).astype(dtype).astype(np.float64)
    return np.moveaxis((codes * scale).reshape(v.shape), -1, axis)


WIDE = False


def mx_kscale(k):
    if not WIDE:
        return np.ones(k)
    levels = np.array([10, -10, 5, -5, 0])
    if k % 512:
        return np.exp2(np.random.permutation(np.resize(levels, k // 32))).repeat(32)
    a = np.empty((k // 512, 16))
    for p in range(k // 512):
        a[p, :8] = np.random.permutation(np.resize(levels, 8))
        for g in range(8):
            far = levels[np.abs(levels - a[p, g]) >= 10]
            a[p, g + 8] = far[np.random.randint(len(far))]
    return np.exp2(a.ravel()).repeat(32)


BF16 = ml_dtypes.bfloat16


def bf(x):
    return np.asarray(x, np.float32).astype(BF16)


def f64(x):
    return np.asarray(x).astype(np.float64)


T, B, R, N = 1024, 1024, 512, 2048

NARROW, BROAD = 0.1, 0.3
SPREAD, MEAN = 4.0, 1.5


def draw0():
    s = mx_kscale(R)
    t = mx_kscale(B)
    phase = np.random.uniform(0.0, 1.0, (T, 1))
    centre = np.random.uniform(0.0, 1.0, (1, B))
    width = np.random.uniform(NARROW, BROAD, (1, B))
    g = np.exp(-0.5 * ((phase - centre) / width) ** 2) / np.sqrt(B)
    factor = SPREAD * np.random.standard_normal((B, R)) / np.sqrt(R)
    noise = np.random.standard_normal((R, N))
    mean = MEAN * np.random.standard_normal(B)
    return {"factor": bf(factor * s * t[:, None]),
            "noise": bf(noise / s[:, None]),
            "mean": bf(mean * t),
            "basis": bf(g / t),
            "rnorm": bf(1.0 / g.sum(axis=1)),
            "amp": bf(1.0 + 0.1 * np.random.standard_normal(N))}


def core(factor, noise, mean, basis, rnorm, amp):
    dev = mxq(f64(factor), 1, "e4m3") @ mxq(f64(noise), 0, "e4m3")
    w = dev + f64(mean)[:, None]
    y = mxq(f64(basis), 1, "e4m3") @ mxq(w, 0, "e4m3")
    return y * f64(rnorm)[:, None] * f64(amp)


def e4m3fn_bytes(y):
    return np.clip(np.asarray(y, np.float64), -448.0, 448.0).astype(np.float32).astype(ml_dtypes.float8_e4m3fn).view(np.uint8)


def e4m3fn_values(b):
    return np.asarray(b, np.uint8).view(ml_dtypes.float8_e4m3fn).astype(np.float64)


def setup_inputs():
    d = draw0()
    x0 = np.asarray(d['noise']).astype(np.float64)
    s = (np.max(np.abs(x0), axis=(1,), keepdims=True) / 448.0).astype(np.float32)
    out = {}
    for k, v in d.items():
        if k == 'noise':
            out['noise_bytes'] = e4m3fn_bytes(x0 / s.astype(np.float64))
            out['noise_scale'] = s
        else:
            out[k] = v
    return out


def reference(factor, noise_bytes, noise_scale, mean, basis, rnorm, amp):
    return core(factor, e4m3fn_values(noise_bytes) * noise_scale.astype(np.float64), mean, basis, rnorm, amp)

@@ -1,0 +1,296 @@
+from contextlib import ExitStack
+
+import concourse.mybir as mybir
+from concourse.masks import make_identity
+
+T, B, R, N = 1024, 1024, 512, 2048
+FLOPS = 2 * B * R * N + 2 * T * B * N
+
+F32 = mybir.dt.float32
+BF16 = mybir.dt.bfloat16
+U32 = mybir.dt.uint32
+U8 = mybir.dt.uint8
+FP8 = mybir.dt.float8_e4m3fn
+FP8X4 = mybir.dt.float8_e4m3fn_x4
+ALU = mybir.AluOpType
+ACT = mybir.ActivationFunctionType
+
+P = 128
+CH = 512
+NCH = N // CH
+HALF = 256
+PLAN = {'pew': [(1, 0, 1), (2, 0, 0), (2, 0, 1), (2, 1, 0), (2, 1, 1), (3, 1, 1)], 'epg': [20, 21, 22, 24, 26], 'inh': -1.77, 'dQ': 1.479, 'dF': -42.52, 'dE': 0.848, 'dIp': -51.048, 'S10': -16.206, 'rS10': 0.952, 'Tf00': -64.304, 'Ef00': -58.227, 'eEf00': 'S', 'Tf01': -53.701, 'Ef01': -74.042, 'eEf01': 'S', 'Tf10': -42.45, 'Ef10': -139.993, 'eEf10': 'S', 'Tf11': -34.666, 'Ef11': -51.932, 'eEf11': 'S', 'qf0': -61.717, 'qf1': -67.426, 'wd0': -120.939, 'in0': -111.952, 'qn0': -43.753, 'ewd0': 'V', 'wd1': -11.271, 'in1': -139.479, 'qn1': -8.985, 'ewd1': 'S', 'wd2': -6.414, 'in2': -38.395, 'qn2': -0.738, 'ewd2': 'S', 'wd3': 6.004, 'in3': 12.547, 'qn3': 7.798, 'ewd3': 'S', 'A11': 9.012, 'r11': 0.501, 'AI1': 6.193, 'rI1': 0.893, 'A12': 11.633, 'r12': 0.274, 'AI2': 2.829, 'rI2': 0.049, 'A13': 9.817, 'r13': 0.545, 'AI3': 7.296, 'rI3': 1.21, 'I00': -50.005, 'Q00': -43.944, 'I01': -64.313, 'Q01': -24.928, 'I02': -62.958, 'Q02': -26.701, 'I03': -65.292, 'Q03': -42.19, 'Tb0': -25.267, 'Eb0': -59.224, 'qb0': -12.676, 'eEb0': 'S', 'Tb1': -22.821, 'Eb1': -21.405, 'qb1': -13.91, 'eEb1': 'S', 'Tb2': -5.309, 'Eb2': -29.382, 'qb2': -20.865, 'eEb2': 'S', 'Tb3': -3.064, 'Eb3': -40.225, 'qb3': -17.997, 'eEb3': 'S', 'Tb4': -6.919, 'Eb4': -57.9, 'qb4': -70.203, 'eEb4': 'S', 'Tb5': -3.426, 'Eb5': -60.723, 'qb5': -76.445, 'eEb5': 'S', 'Tb6': 3.905, 'Eb6': -31.57, 'qb6': -29.211, 'eEb6': 'S', 'Tb7': 4.326, 'Eb7': -103.353, 'qb7': -7.608, 'eEb7': 'S', 'eE10': 'V', 'eE11': 'S', 'eE12': 'V', 'eE13': 'S', 'eE14': 'V', 'eE15': 'S', 'eE16': 'V', 'eE17': 'S', 'na': 5, 'nb': 3}
+
+
+def tile_promp_trajectory_sampling_s7_kernel(tc, factor, noise_bytes, noise_scale, mean, basis, rnorm, amp, out):
+    nc = tc.nc
+    with ExitStack() as ctx:
+        keep = ctx.enter_context(tc.tile_pool(name="keep", bufs=1))
+        stage = ctx.enter_context(tc.tile_pool(name="stage", bufs=2))
+        psum = ctx.enter_context(tc.psum_pool(name="psum", bufs=PLAN["na"]))
+        psum2 = ctx.enter_context(tc.psum_pool(name="psum2", bufs=PLAN["nb"]))
+        ident_b = ctx.enter_context(tc.tile_pool(name="idb", bufs=1)).tile([P, P], BF16, name="ident_b")
+
+        ident = keep.tile([P, P], F32, name="ident")
+        dummy = keep.tile([P, 1], F32, name="dummy")
+        nscale = keep.tile([P, 4], F32, name="nscale")
+        mean_b = keep.tile([P, 2, 4], BF16, name="mean_b")
+        mean_f = keep.tile([P, 2, 4], F32, name="mean_f")
+        rn_b = keep.tile([P, 8], BF16, name="rn_b")
+        rn_f = keep.tile([P, 8], F32, name="rn_f")
+        amp_b = keep.tile([P, N], BF16, name="amp_b")
+        fac_rows = keep.tile([P, 2, 4, R], BF16, name="fac_rows")
+        fac_k = keep.tile([P, 2, 4, P, 4], BF16, name="fac_k", align_bytes=64)
+        fac_q = keep.tile([P, 2, 4 * P], U32, name="fac_q", align_bytes=64)
+        fac_s = keep.tile([P, 2, 4 * P], U8, name="fac_s", align_bytes=64)
+        bas_rows = keep.tile([P, 8, B], BF16, name="bas_rows")
+        bas_k = keep.tile([P, 8, 2, P, 4], BF16, name="bas_k", align_bytes=64)
+        bas_q = keep.tile([P, 8, 2 * P], U32, name="bas_q", align_bytes=64)
+        bas_s = keep.tile([P, 8, 2 * P], U8, name="bas_s", align_bytes=64)
+        nz_bytes = keep.tile([P, NCH, 4, CH], U8, name="nz_bytes")
+        nz_q = keep.tile([P, NCH, CH], U32, name="nz_q", align_bytes=64)
+        nz_s = keep.tile([P, NCH, CH], U8, name="nz_s", align_bytes=64)
+
+        fac_v = factor.rearrange("(g m t) k -> g m t k", g=2, t=4)
+        nz_v = noise_bytes.rearrange("(p t) (c n) -> c p t n", t=4, n=CH)
+        bas_v = basis.rearrange("(p n) b -> p n b", n=8)
+        out_v = out.rearrange("(p n) j -> p n j", n=8)
+
+        nc.scalar.dma_start(out=nscale[:], in_=noise_scale.rearrange("(p t) o -> p (t o)", t=4))
+        nc.scalar.dma_start(out=mean_b[:], in_=mean.rearrange("(g p t) -> p g t", g=2, t=4))
+        nc.scalar.dma_start(out=rn_b[:], in_=rnorm.rearrange("(p n) -> p n", n=8))
+
+        def load_fac(g, h):
+            nc.sync.dma_start(out=fac_rows[:, g, 2 * h : 2 * h + 2, :], in_=fac_v[g][:, 2 * h : 2 * h + 2, :])
+
+        def load_nz(c):
+            nc.sync.dma_start(out=nz_bytes[:, c], in_=nz_v[c])
+
+        def load_bas(n):
+            nc.sync.dma_start(out=bas_rows[:, n : n + 2, :], in_=bas_v[:, n : n + 2, :])
+
+        load_fac(0, 0)
+        load_nz(0)
+        load_fac(0, 1)
+        load_fac(1, 0)
+        load_fac(1, 1)
+        load_bas(0)
+        load_nz(1)
+        load_bas(2)
+        load_nz(2)
+        load_bas(4)
+        load_bas(6)
+        load_nz(3)
+        nc.sync.dma_start(out=amp_b[:], in_=amp.partition_broadcast(P))
+
+        make_identity(nc, ident[:])
+        if PLAN['pew']:
+            nc.vector.tensor_copy(out=ident_b[:], in_=ident[:])
+        nc.vector.memset(dummy[:], 0.0)
+        nc.scalar.activation(out=dummy[:], in_=dummy[:], func=ACT.Identity)
+
+        fac_w = fac_rows[:].bitcast(F32)
+        bas_w = bas_rows[:].bitcast(F32)
+
+        def turn_factor(g, h):
+            bank = psum.tile([P, CH], F32, name="bank")
+            for a in range(2):
+                for u in range(2):
+                    nc.tensor.transpose(bank[:, P * (2 * a + u) : P * (2 * a + u + 1)], fac_w[:, g, 2 * h + a, u::2], ident[:])
+            return bank
+
+        def empty_factor(e, bank, g, h):
+            eng = nc.scalar.copy if e == 'S' else nc.vector.tensor_copy
+            o = fac_k[:, g, 2 * h : 2 * h + 2].rearrange("p a r t -> p (a r t)").bitcast(F32)
+            eng(out=o.rearrange("p (a r u) -> p a r u", a=2, u=2), in_=bank[:].rearrange("p (a u r) -> p a r u", a=2, u=2))
+
+        def quant_factor(g):
+            nc.vector.quantize_mx(out=fac_q[:, g].bitcast(FP8X4), scales=fac_s[:, g], in_=fac_k[:, g].rearrange("p t r i -> p (t r i)"))
+
+        def turn_basis(n):
+            bank = psum.tile([P, CH], F32, name="bank")
+            for g in range(2):
+                for u in range(2):
+                    nc.tensor.transpose(bank[:, P * (2 * g + u) : P * (2 * g + u + 1)], bas_w[:, n, 256 * g + u : 256 * (g + 1) : 2], ident[:])
+            return bank
+
+        def empty_basis(e, bank, n):
+            eng = nc.scalar.copy if e == 'S' else nc.vector.tensor_copy
+            o = bas_k[:, n].rearrange("p g r t -> p (g r t)").bitcast(F32)
+            eng(out=o.rearrange("p (g r u) -> p g r u", g=2, u=2), in_=bank[:].rearrange("p (g u r) -> p g r u", g=2, u=2))
+
+        def quant_basis(n):
+            nc.vector.quantize_mx(out=bas_q[:, n].bitcast(FP8X4), scales=bas_s[:, n], in_=bas_k[:, n].rearrange("p g r i -> p (g r i)"))
+
+
+        def A(name):
+            return PLAN[name]
+
+        work = []
+        keys = {}
+
+        def at(step, name, deps, job, *args):
+            step = max([step] + [keys[d] + 0.0001 for d in deps])
+            keys[name] = step
+            work.append((step, len(work), job, args))
+
+        bk = {}
+        planes = {}
+        woven = {}
+        w_planes = {}
+        w_woven = {}
+        w_q = {}
+        w_s = {}
+        res = {}
+        half = {}
+
+        def j_tf(g, h):
+            bk["f", g, h] = turn_factor(g, h)
+
+        def j_ef(e, g, h):
+            empty_factor(e, bk["f", g, h], g, h)
+
+        def j_tb(n):
+            bk["b", n] = turn_basis(n)
+
+        def j_eb(e, n):
+            empty_basis(e, bk["b", n], n)
+
+        def j_wd(e, c, t):
+            if c not in planes:
+                planes[c] = stage.tile([P, 4, CH], BF16, name="nz_planes", bufs=3)
+            src = nz_bytes[:, c, t, :].bitcast(FP8)
+            if e == "S":
+                nc.scalar.activation(out=planes[c][:, t, :], in_=src, func=ACT.Copy, scale=nscale[:, t : t + 1])
+            else:
+                nc.vector.tensor_scalar(out=planes[c][:, t, :], in0=src, scalar1=nscale[:, t : t + 1], scalar2=None, op0=ALU.mult)
+
+        def interleave(dst, src):
+            nc.vector.tensor_copy(out=dst.rearrange("p (c i) t -> p c t i", i=4), in_=src.rearrange("p t (c i) -> p c t i", i=4))
+
+        def j_in(c, h):
+            if c not in woven:
+                woven[c] = stage.tile([P, CH, 4], BF16, name="nz_woven", align_bytes=64, bufs=3)
+            cols = slice(HALF * h, HALF * (h + 1))
+            interleave(woven[c][:, cols, :], planes[c][:, :, cols])
+
+        def j_qn(c):
+            nc.vector.quantize_mx(out=nz_q[:, c].bitcast(FP8X4), scales=nz_s[:, c], in_=woven[c][:].rearrange("p n t -> p (n t)"))
+
+        def j_s1(c, g, t):
+            bank = psum.tile([P, CH], F32, name="bank")
+            bk["w", c, g, t] = bank
+            nc.tensor.matmul_mx(out=bank[:], lhsT=fac_q[:, g, P * t : P * (t + 1)].bitcast(FP8X4), lhsT_scale=fac_s[:, g, P * t : P * (t + 1)],
+                                rhs=nz_q[:, c].bitcast(FP8X4), rhs_scale=nz_s[:, c], start=True, stop=True)
+
+        def j_e1(e, c, g, t):
+            if (c, g) not in w_planes:
+                w_planes[c, g] = stage.tile([P, 4, CH], BF16, name="w_planes", bufs=4)
+            o = w_planes[c, g][:, t, :]
+            b = bk["w", c, g, t]
+            if e == "S":
+                nc.scalar.activation(out=o, in_=b[:], func=ACT.Identity, bias=mean_f[:, g, t : t + 1])
+            else:
+                nc.vector.tensor_scalar(out=o, in0=b[:], scalar1=mean_f[:, g, t : t + 1], scalar2=None, op0=ALU.add)
+
+        def w_tile(c, g):
+            if (c, g) not in w_woven:
+                w_woven[c, g] = stage.tile([P, CH, 4], BF16, name="w_woven", align_bytes=64, bufs=4)
+            return w_woven[c, g]
+
+        def j_i(c, g, h):
+            cols = slice(HALF * h, HALF * (h + 1))
+            interleave(w_tile(c, g)[:, cols, :], w_planes[c, g][:, :, cols])
+
+        def j_ip(c, g, h):
+            bank = psum.tile([P, 4 * HALF], BF16, name="bank")
+            bk["i", c, g, h] = bank
+            for k in range(2):
+                cols = slice(HALF * h + P * k, HALF * h + P * (k + 1))
+                nc.tensor.matmul(bank[:, CH * k : CH * (k + 1)], lhsT=ident_b[:], rhs=w_planes[c, g][:, :, cols].rearrange("p t n -> p n t"), start=True, stop=True)
+
+        def j_is(c, g, h):
+            cols = slice(HALF * h, HALF * (h + 1))
+            nc.scalar.copy(out=w_tile(c, g)[:, cols, :].rearrange("p n t -> p (n t)"), in_=bk["i", c, g, h][:])
+
+        def j_q(c, g, h):
+            if (c, g) not in w_q:
+                w_q[c, g] = stage.tile([P, CH], U32, name="w_q", align_bytes=64, bufs=6)
+                w_s[c, g] = stage.tile([P, CH], U8, name="w_s", align_bytes=64, bufs=6)
+            cols = slice(HALF * h, HALF * (h + 1))
+            nc.vector.quantize_mx(out=w_q[c, g][:, cols].bitcast(FP8X4), scales=w_s[c, g][:, cols], in_=w_woven[c, g][:, cols, :].rearrange("p n t -> p (n t)"))
+
+        def j_s2(s):
+            c, n = divmod(s, 8)
+            bank = psum2.tile([P, CH], F32, name="sum")
+            bk["y", s] = bank
+            for g in range(2):
+                cols = slice(P * g, P * (g + 1))
+                nc.tensor.matmul_mx(out=bank[:], lhsT=bas_q[:, n, cols].bitcast(FP8X4), lhsT_scale=bas_s[:, n, cols],
+                                    rhs=w_q[c, g][:].bitcast(FP8X4), rhs_scale=w_s[c, g][:], start=(g == 0), stop=(g == 1))
+
+        def j_y(s):
+            n = s % 8
+            half[s] = stage.tile([P, CH], F32, name="half_done", bufs=3)
+            nc.scalar.activation(out=half[s][:], in_=bk["y", s][:], func=ACT.Copy, scale=rn_f[:, n : n + 1])
+
+        def j_f(e, s):
+            c, n = divmod(s, 8)
+            if s // 2 not in res:
+                res[s // 2] = stage.tile([P, 2, CH], F32, name="res", bufs=5)
+            o = res[s // 2][:, n % 2, :]
+            a = amp_b[:, CH * c : CH * (c + 1)]
+            if e == "G":
+                nc.gpsimd.tensor_tensor(out=o, in0=half[s][:], in1=a, op=ALU.mult)
+            else:
+                nc.vector.scalar_tensor_tensor(out=o, in0=bk["y", s][:], scalar=rn_f[:, n : n + 1], in1=a, op0=ALU.mult, op1=ALU.mult)
+            if s >= 30:
+                nc.sync.dma_start(out=out_v[:, n, CH * c : CH * (c + 1)], in_=o)
+            elif n % 2 == 1:
+                nc.sync.dma_start(out=out_v[:, n - 1 : n + 1, CH * c : CH * (c + 1)], in_=res[s // 2][:])
+
+        for g in range(2):
+            for h in range(2):
+                at(A(f"Tf{g}{h}"), ("Tf", g, h), [], j_tf, g, h)
+                at(A(f"Ef{g}{h}"), ("Ef", g, h), [("Tf", g, h)], j_ef, A(f"eEf{g}{h}"), g, h)
+            at(A(f"qf{g}"), ("qf", g), [("Ef", g, 0), ("Ef", g, 1)], quant_factor, g)
+        for n in range(8):
+            at(A(f"Tb{n}"), ("Tb", n), [], j_tb, n)
+            at(A(f"Eb{n}"), ("Eb", n), [("Tb", n)], j_eb, A(f"eEb{n}"), n)
+            at(A(f"qb{n}"), ("qb", n), [("Eb", n)], quant_basis, n)
+        for c in range(NCH):
+            for t in range(4):
+                at(A(f"wd{c}") + t * 0.01, ("wd", c, t), [], j_wd, A(f"ewd{c}"), c, t)
+            for h in range(2):
+                at(A(f"in{c}") + h * A("inh"), ("in", c, h), [("wd", c, t) for t in range(4)], j_in, c, h)
+            at(A(f"qn{c}"), ("qn", c), [("in", c, 0), ("in", c, 1)], j_qn, c)
+            for u in range(8):
+                g, t = divmod(u, 4)
+                k = A("S10") + u * A("rS10") if c == 0 else 8 * c - A(f"A1{c}") + u * A(f"r1{c}")
+                at(k, ("S1", c, g, t), [("qn", c), ("qf", g)], j_s1, c, g, t)
+                at(k + A("dE"), ("E1", c, g, t), [("S1", c, g, t)], j_e1, A(f"eE1{u}") if c == 0 else "S", c, g, t)
+            for i in range(4):
+                g, h = divmod(i, 2)
+                k = A(f"I0{i}") if c == 0 else 8 * c - A(f"AI{c}") + i * A(f"rI{c}")
+                e1 = [("E1", c, g, t) for t in range(4)]
+                if (c, g, h) in A("pew"):
+                    at(k, ("Ip", c, g, h), e1, j_ip, c, g, h)
+                    at(k + A("dIp"), ("I", c, g, h), [("Ip", c, g, h)], j_is, c, g, h)
+                    at(k + A("dIp") + A("dQ"), ("Q", c, g, h), [("I", c, g, h)], j_q, c, g, h)
+                else:
+                    at(k, ("I", c, g, h), e1, j_i, c, g, h)
+                    at(A(f"Q0{i}") if c == 0 else k + A("dQ"), ("Q", c, g, h), [("I", c, g, h)], j_q, c, g, h)
+        for s in range(8 * NCH):
+            c, n = divmod(s, 8)
+            at(s, ("S2", s), [("qb", n)] + [("Q", c, g, h) for g in range(2) for h in range(2)], j_s2, s)
+            if s in A("epg"):
+                at(s + A("dF"), ("Y", s), [("S2", s)], j_y, s)
+                at(s + A("dF"), ("F", s), [("Y", s)], j_f, "G", s)
+            else:
+                at(s + A("dF"), ("F", s), [("S2", s)], j_f, "V", s)
+
+        with tc.manual_schedule():
+            nc.vector.tensor_copy(out=mean_f[:], in_=mean_b[:])
+            nc.vector.tensor_copy(out=rn_f[:], in_=rn_b[:])
+            for step, order, job, args in sorted(work, key=lambda w: w[:2]):
+                job(*args)

@@ -19,7 +19,7 @@ P = 128
 CH = 512
 NCH = N // CH
 HALF = 256
-PLAN = {'pew': [(1, 0, 1), (2, 0, 0), (2, 0, 1), (2, 1, 0), (2, 1, 1), (3, 1, 1)], 'epg': [20, 21, 22, 24, 26], 'inh': -1.77, 'dQ': 1.479, 'dF': -42.52, 'dE': 0.848, 'dIp': -51.048, 'S10': -16.206, 'rS10': 0.952, 'Tf00': -64.304, 'Ef00': -58.227, 'eEf00': 'S', 'Tf01': -53.701, 'Ef01': -74.042, 'eEf01': 'S', 'Tf10': -42.45, 'Ef10': -139.993, 'eEf10': 'S', 'Tf11': -34.666, 'Ef11': -51.932, 'eEf11': 'S', 'qf0': -61.717, 'qf1': -67.426, 'wd0': -120.939, 'in0': -111.952, 'qn0': -43.753, 'ewd0': 'V', 'wd1': -11.271, 'in1': -139.479, 'qn1': -8.985, 'ewd1': 'S', 'wd2': -6.414, 'in2': -38.395, 'qn2': -0.738, 'ewd2': 'S', 'wd3': 6.004, 'in3': 12.547, 'qn3': 7.798, 'ewd3': 'S', 'A11': 9.012, 'r11': 0.501, 'AI1': 6.193, 'rI1': 0.893, 'A12': 11.633, 'r12': 0.274, 'AI2': 2.829, 'rI2': 0.049, 'A13': 9.817, 'r13': 0.545, 'AI3': 7.296, 'rI3': 1.21, 'I00': -50.005, 'Q00': -43.944, 'I01': -64.313, 'Q01': -24.928, 'I02': -62.958, 'Q02': -26.701, 'I03': -65.292, 'Q03': -42.19, 'Tb0': -25.267, 'Eb0': -59.224, 'qb0': -12.676, 'eEb0': 'S', 'Tb1': -22.821, 'Eb1': -21.405, 'qb1': -13.91, 'eEb1': 'S', 'Tb2': -5.309, 'Eb2': -29.382, 'qb2': -20.865, 'eEb2': 'S', 'Tb3': -3.064, 'Eb3': -40.225, 'qb3': -17.997, 'eEb3': 'S', 'Tb4': -6.919, 'Eb4': -57.9, 'qb4': -70.203, 'eEb4': 'S', 'Tb5': -3.426, 'Eb5': -60.723, 'qb5': -76.445, 'eEb5': 'S', 'Tb6': 3.905, 'Eb6': -31.57, 'qb6': -29.211, 'eEb6': 'S', 'Tb7': 4.326, 'Eb7': -103.353, 'qb7': -7.608, 'eEb7': 'S', 'eE10': 'V', 'eE11': 'S', 'eE12': 'V', 'eE13': 'S', 'eE14': 'V', 'eE15': 'S', 'eE16': 'V', 'eE17': 'S', 'na': 5, 'nb': 3}
+PLAN = {'epg': [], 'inh': -39.051, 'dQ': 0.167, 'dF': -51.338, 'dE': -124.049, 'S10': -38.549, 'rS10': 0.274, 'Tf00': -111.447, 'Ef00': -102.882, 'eEf00': 'V', 'Tf01': -64.202, 'Ef01': -67.941, 'eEf01': 'S', 'Tf10': -62.312, 'Ef10': -119.012, 'eEf10': 'S', 'Tf11': -54.81, 'Ef11': -95.031, 'eEf11': 'S', 'qf0': -112.848, 'qf1': -87.952, 'wd0': -126.004, 'in0': -210.408, 'qn0': -82.001, 'ewd0': 'V', 'wd1': -51.98, 'in1': -134.756, 'qn1': -20.034, 'ewd1': 'S', 'wd2': -29.165, 'in2': -29.245, 'qn2': -2.351, 'ewd2': 'S', 'wd3': 4.595, 'in3': 9.099, 'qn3': 6.058, 'ewd3': 'S', 'A11': 7.722, 'r11': 0.61, 'AI1': 93.026, 'rI1': -56.369, 'A12': 11.477, 'r12': 0.503, 'AI2': 4.0, 'rI2': 0.003, 'A13': 11.662, 'r13': 0.264, 'AI3': 3.317, 'rI3': 0.24, 'I00': -94.079, 'Q00': -208.364, 'I01': -43.089, 'Q01': -42.011, 'I02': -97.486, 'Q02': -20.102, 'I03': -167.28, 'Q03': -209.794, 'Tb0': -24.903, 'Eb0': -24.713, 'qb0': -41.119, 'eEb0': 'S', 'Tb1': -6.382, 'Eb1': -219.428, 'qb1': -40.094, 'eEb1': 'S', 'Tb2': -4.425, 'Eb2': -72.769, 'qb2': -96.515, 'eEb2': 'S', 'Tb3': -1.241, 'Eb3': -93.011, 'qb3': -76.132, 'eEb3': 'S', 'Tb4': -19.536, 'Eb4': -60.424, 'qb4': -49.696, 'eEb4': 'S', 'Tb5': -3.771, 'Eb5': -162.04, 'qb5': -66.674, 'eEb5': 'S', 'Tb6': 2.541, 'Eb6': -84.057, 'qb6': -29.251, 'eEb6': 'S', 'Tb7': -0.195, 'Eb7': -5.304, 'qb7': -212.351, 'eEb7': 'S', 'eE10': 'S', 'eE11': 'V', 'eE12': 'S', 'eE13': 'V', 'eE14': 'S', 'eE15': 'S', 'eE16': 'S', 'eE17': 'S', 'sn': {(1, 0): 'G', (1, 1): 'G', (2, 0): 'G', (2, 1): 'S', (3, 0): 'G'}, 'dEA': -50.122, 'SA': 20.991, 'na': 5, 'nb': 3, 'iw': {(2, 0, 0): 'S', (2, 0, 1): 'G', (2, 1, 0): 'G', (3, 0, 0): 'G', (3, 0, 1): 'S', (3, 1, 0): 'S', (3, 1, 1): 'G'}, 'fused': [(0, 0), (0, 1)]}
 
 
 def tile_promp_trajectory_sampling_s7_kernel(tc, factor, noise_bytes, noise_scale, mean, basis, rnorm, amp, out):
@@ -29,7 +29,6 @@ def tile_promp_trajectory_sampling_s7_kernel(tc, factor, noise_bytes, noise_scal
         stage = ctx.enter_context(tc.tile_pool(name="stage", bufs=2))
         psum = ctx.enter_context(tc.psum_pool(name="psum", bufs=PLAN["na"]))
         psum2 = ctx.enter_context(tc.psum_pool(name="psum2", bufs=PLAN["nb"]))
-        ident_b = ctx.enter_context(tc.tile_pool(name="idb", bufs=1)).tile([P, P], BF16, name="ident_b")
 
         ident = keep.tile([P, P], F32, name="ident")
         dummy = keep.tile([P, 1], F32, name="dummy")
@@ -69,8 +68,9 @@ def tile_promp_trajectory_sampling_s7_kernel(tc, factor, noise_bytes, noise_scal
         def load_bas(n):
             nc.sync.dma_start(out=bas_rows[:, n : n + 2, :], in_=bas_v[:, n : n + 2, :])
 
+        for h in range(2):
+            nc.sync.dma_start(out=nz_bytes[:, 0, 2 * h : 2 * h + 2], in_=nz_v[0][:, 2 * h : 2 * h + 2])
         load_fac(0, 0)
-        load_nz(0)
         load_fac(0, 1)
         load_fac(1, 0)
         load_fac(1, 1)
@@ -84,8 +84,6 @@ def tile_promp_trajectory_sampling_s7_kernel(tc, factor, noise_bytes, noise_scal
         nc.sync.dma_start(out=amp_b[:], in_=amp.partition_broadcast(P))
 
         make_identity(nc, ident[:])
-        if PLAN['pew']:
-            nc.vector.tensor_copy(out=ident_b[:], in_=ident[:])
         nc.vector.memset(dummy[:], 0.0)
         nc.scalar.activation(out=dummy[:], in_=dummy[:], func=ACT.Identity)
 
@@ -165,14 +163,21 @@ def tile_promp_trajectory_sampling_s7_kernel(tc, factor, noise_bytes, noise_scal
             else:
                 nc.vector.tensor_scalar(out=planes[c][:, t, :], in0=src, scalar1=nscale[:, t : t + 1], scalar2=None, op0=ALU.mult)
 
-        def interleave(dst, src):
-            nc.vector.tensor_copy(out=dst.rearrange("p (c i) t -> p c t i", i=4), in_=src.rearrange("p t (c i) -> p c t i", i=4))
+        def interleave(e, dst, src):
+            d = dst.rearrange("p (c i) t -> p c t i", i=4)
+            s = src.rearrange("p t (c i) -> p c t i", i=4)
+            if e == "S":
+                nc.scalar.copy(out=d, in_=s)
+            elif e == "G":
+                nc.gpsimd.tensor_scalar(out=dst, in0=src.rearrange("p t n -> p n t"), scalar1=1.0, scalar2=0.0, op0=ALU.mult, op1=ALU.add)
+            else:
+                nc.vector.tensor_copy(out=d, in_=s)
 
-        def j_in(c, h):
+        def j_in(e, c, h):
             if c not in woven:
                 woven[c] = stage.tile([P, CH, 4], BF16, name="nz_woven", align_bytes=64, bufs=3)
             cols = slice(HALF * h, HALF * (h + 1))
-            interleave(woven[c][:, cols, :], planes[c][:, :, cols])
+            interleave(e, woven[c][:, cols, :], planes[c][:, :, cols])
 
         def j_qn(c):
             nc.vector.quantize_mx(out=nz_q[:, c].bitcast(FP8X4), scales=nz_s[:, c], in_=woven[c][:].rearrange("p n t -> p (n t)"))
@@ -193,25 +198,27 @@ def tile_promp_trajectory_sampling_s7_kernel(tc, factor, noise_bytes, noise_scal
             else:
                 nc.vector.tensor_scalar(out=o, in0=b[:], scalar1=mean_f[:, g, t : t + 1], scalar2=None, op0=ALU.add)
 
+        def j_s1f(c, g, blk):
+            bank = psum.tile([P, CH], F32, name="bank")
+            bk["w", c, g, blk] = bank
+            cols = slice(P * blk, P * (blk + 1))
+            for t in range(4):
+                nc.tensor.matmul_mx(out=bank[:, P * t : P * (t + 1)], lhsT=fac_q[:, g, P * t : P * (t + 1)].bitcast(FP8X4), lhsT_scale=fac_s[:, g, P * t : P * (t + 1)],
+                                    rhs=nz_q[:, c, cols].bitcast(FP8X4), rhs_scale=nz_s[:, c, cols], start=True, stop=True)
+
+        def j_e1f(c, g, blk):
+            o = w_tile(c, g)[:, P * blk : P * (blk + 1), :]
+            m = mean_f[:, g, :].unsqueeze(1).to_broadcast([P, P, 4])
+            nc.vector.tensor_tensor(out=o, in0=bk["w", c, g, blk][:].rearrange("p (t n) -> p n t", t=4), in1=m, op=ALU.add)
+
         def w_tile(c, g):
             if (c, g) not in w_woven:
                 w_woven[c, g] = stage.tile([P, CH, 4], BF16, name="w_woven", align_bytes=64, bufs=4)
             return w_woven[c, g]
 
-        def j_i(c, g, h):
+        def j_i(e, c, g, h):
             cols = slice(HALF * h, HALF * (h + 1))
-            interleave(w_tile(c, g)[:, cols, :], w_planes[c, g][:, :, cols])
-
-        def j_ip(c, g, h):
-            bank = psum.tile([P, 4 * HALF], BF16, name="bank")
-            bk["i", c, g, h] = bank
-            for k in range(2):
-                cols = slice(HALF * h + P * k, HALF * h + P * (k + 1))
-                nc.tensor.matmul(bank[:, CH * k : CH * (k + 1)], lhsT=ident_b[:], rhs=w_planes[c, g][:, :, cols].rearrange("p t n -> p n t"), start=True, stop=True)
-
-        def j_is(c, g, h):
-            cols = slice(HALF * h, HALF * (h + 1))
-            nc.scalar.copy(out=w_tile(c, g)[:, cols, :].rearrange("p n t -> p (n t)"), in_=bk["i", c, g, h][:])
+            interleave(e, w_tile(c, g)[:, cols, :], w_planes[c, g][:, :, cols])
 
         def j_q(c, g, h):
             if (c, g) not in w_q:
@@ -222,7 +229,10 @@ def tile_promp_trajectory_sampling_s7_kernel(tc, factor, noise_bytes, noise_scal
 
         def j_s2(s):
             c, n = divmod(s, 8)
-            bank = psum2.tile([P, CH], F32, name="sum")
+            if s >= A("SA") and s % 2:
+                bank = psum.tile([P, CH], F32, name="bank")
+            else:
+                bank = psum2.tile([P, CH], F32, name="sum")
             bk["y", s] = bank
             for g in range(2):
                 cols = slice(P * g, P * (g + 1))
@@ -262,23 +272,25 @@ def tile_promp_trajectory_sampling_s7_kernel(tc, factor, noise_bytes, noise_scal
             for t in range(4):
                 at(A(f"wd{c}") + t * 0.01, ("wd", c, t), [], j_wd, A(f"ewd{c}"), c, t)
             for h in range(2):
-                at(A(f"in{c}") + h * A("inh"), ("in", c, h), [("wd", c, t) for t in range(4)], j_in, c, h)
+                at(A(f"in{c}") + h * A("inh"), ("in", c, h), [("wd", c, t) for t in range(4)], j_in, A("sn").get((c, h), "V"), c, h)
             at(A(f"qn{c}"), ("qn", c), [("in", c, 0), ("in", c, 1)], j_qn, c)
             for u in range(8):
                 g, t = divmod(u, 4)
                 k = A("S10") + u * A("rS10") if c == 0 else 8 * c - A(f"A1{c}") + u * A(f"r1{c}")
+                if (c, g) in A("fused"):
+                    at(k, ("S1", c, g, t), [("qn", c), ("qf", g)], j_s1f, c, g, t)
+                    at(k + A("dEA"), ("E1", c, g, t), [("S1", c, g, t)], j_e1f, c, g, t)
+                    continue
                 at(k, ("S1", c, g, t), [("qn", c), ("qf", g)], j_s1, c, g, t)
                 at(k + A("dE"), ("E1", c, g, t), [("S1", c, g, t)], j_e1, A(f"eE1{u}") if c == 0 else "S", c, g, t)
             for i in range(4):
                 g, h = divmod(i, 2)
                 k = A(f"I0{i}") if c == 0 else 8 * c - A(f"AI{c}") + i * A(f"rI{c}")
                 e1 = [("E1", c, g, t) for t in range(4)]
-                if (c, g, h) in A("pew"):
-                    at(k, ("Ip", c, g, h), e1, j_ip, c, g, h)
-                    at(k + A("dIp"), ("I", c, g, h), [("Ip", c, g, h)], j_is, c, g, h)
-                    at(k + A("dIp") + A("dQ"), ("Q", c, g, h), [("I", c, g, h)], j_q, c, g, h)
+                if (c, g) in A("fused"):
+                    at(A(f"Q0{i}") if c == 0 else k + A("dQ"), ("Q", c, g, h), [("E1", c, g, 2 * h), ("E1", c, g, 2 * h + 1)], j_q, c, g, h)
                 else:
-                    at(k, ("I", c, g, h), e1, j_i, c, g, h)
+                    at(k, ("I", c, g, h), e1, j_i, A("iw").get((c, g, h), "V"), c, g, h)
                     at(A(f"Q0{i}") if c == 0 else k + A("dQ"), ("Q", c, g, h), [("I", c, g, h)], j_q, c, g, h)
         for s in range(8 * NCH):
             c, n = divmod(s, 8)

@@ -19,7 +19,7 @@ P = 128
 CH = 512
 NCH = N // CH
 HALF = 256
-PLAN = {'epg': [], 'inh': -39.051, 'dQ': 0.167, 'dF': -51.338, 'dE': -124.049, 'S10': -38.549, 'rS10': 0.274, 'Tf00': -111.447, 'Ef00': -102.882, 'eEf00': 'V', 'Tf01': -64.202, 'Ef01': -67.941, 'eEf01': 'S', 'Tf10': -62.312, 'Ef10': -119.012, 'eEf10': 'S', 'Tf11': -54.81, 'Ef11': -95.031, 'eEf11': 'S', 'qf0': -112.848, 'qf1': -87.952, 'wd0': -126.004, 'in0': -210.408, 'qn0': -82.001, 'ewd0': 'V', 'wd1': -51.98, 'in1': -134.756, 'qn1': -20.034, 'ewd1': 'S', 'wd2': -29.165, 'in2': -29.245, 'qn2': -2.351, 'ewd2': 'S', 'wd3': 4.595, 'in3': 9.099, 'qn3': 6.058, 'ewd3': 'S', 'A11': 7.722, 'r11': 0.61, 'AI1': 93.026, 'rI1': -56.369, 'A12': 11.477, 'r12': 0.503, 'AI2': 4.0, 'rI2': 0.003, 'A13': 11.662, 'r13': 0.264, 'AI3': 3.317, 'rI3': 0.24, 'I00': -94.079, 'Q00': -208.364, 'I01': -43.089, 'Q01': -42.011, 'I02': -97.486, 'Q02': -20.102, 'I03': -167.28, 'Q03': -209.794, 'Tb0': -24.903, 'Eb0': -24.713, 'qb0': -41.119, 'eEb0': 'S', 'Tb1': -6.382, 'Eb1': -219.428, 'qb1': -40.094, 'eEb1': 'S', 'Tb2': -4.425, 'Eb2': -72.769, 'qb2': -96.515, 'eEb2': 'S', 'Tb3': -1.241, 'Eb3': -93.011, 'qb3': -76.132, 'eEb3': 'S', 'Tb4': -19.536, 'Eb4': -60.424, 'qb4': -49.696, 'eEb4': 'S', 'Tb5': -3.771, 'Eb5': -162.04, 'qb5': -66.674, 'eEb5': 'S', 'Tb6': 2.541, 'Eb6': -84.057, 'qb6': -29.251, 'eEb6': 'S', 'Tb7': -0.195, 'Eb7': -5.304, 'qb7': -212.351, 'eEb7': 'S', 'eE10': 'S', 'eE11': 'V', 'eE12': 'S', 'eE13': 'V', 'eE14': 'S', 'eE15': 'S', 'eE16': 'S', 'eE17': 'S', 'sn': {(1, 0): 'G', (1, 1): 'G', (2, 0): 'G', (2, 1): 'S', (3, 0): 'G'}, 'dEA': -50.122, 'SA': 20.991, 'na': 5, 'nb': 3, 'iw': {(2, 0, 0): 'S', (2, 0, 1): 'G', (2, 1, 0): 'G', (3, 0, 0): 'G', (3, 0, 1): 'S', (3, 1, 0): 'S', (3, 1, 1): 'G'}, 'fused': [(0, 0), (0, 1)]}
+PLAN = {'epg': [], 'inh': -86.539, 'dQ': -14.564, 'dF': -14.488, 'dE': -121.021, 'S10': -91.812, 'rS10': 3.092, 'Tf00': -196.155, 'Ef00': -164.646, 'eEf00': 'S', 'Tf01': -130.886, 'Ef01': -142.394, 'eEf01': 'S', 'Tf10': -129.331, 'Ef10': -118.99, 'eEf10': 'S', 'Tf11': -117.046, 'Ef11': -137.297, 'eEf11': 'V', 'qf0': -140.053, 'qf1': -149.502, 'wd0': -165.235, 'in0': -302.469, 'qn0': -130.987, 'ewd0': 'V', 'wd1': -49.887, 'in1': -276.174, 'qn1': -131.883, 'ewd1': 'S', 'wd2': -37.534, 'in2': -39.696, 'qn2': -11.086, 'ewd2': 'S', 'wd3': 4.297, 'in3': 10.997, 'qn3': -41.618, 'ewd3': 'S', 'A11': 13.941, 'r11': 1.242, 'AI1': 69.313, 'rI1': -98.495, 'A12': 13.083, 'r12': 0.779, 'AI2': 2.465, 'rI2': -0.201, 'A13': 9.781, 'r13': 0.286, 'AI3': 3.077, 'rI3': 0.313, 'I00': -110.556, 'Q00': -134.424, 'I01': 148.869, 'Q01': -25.98, 'I02': 10.641, 'Q02': -98.864, 'I03': -238.389, 'Q03': -231.086, 'Tb0': -12.674, 'Eb0': -60.812, 'qb0': -85.051, 'eEb0': 'S', 'Tb1': -10.849, 'Eb1': -175.241, 'qb1': -40.442, 'eEb1': 'S', 'Tb2': -10.483, 'Eb2': -49.954, 'qb2': -192.993, 'eEb2': 'S', 'Tb3': -34.225, 'Eb3': -68.496, 'qb3': -29.812, 'eEb3': 'S', 'Tb4': -15.149, 'Eb4': -58.666, 'qb4': -116.279, 'eEb4': 'S', 'Tb5': -30.034, 'Eb5': -74.803, 'qb5': -2.497, 'eEb5': 'S', 'Tb6': -7.4, 'Eb6': -201.352, 'qb6': -106.916, 'eEb6': 'S', 'Tb7': -8.654, 'Eb7': -118.854, 'qb7': -186.722, 'eEb7': 'S', 'eE10': 'S', 'eE11': 'V', 'eE12': 'S', 'eE13': 'V', 'eE14': 'S', 'eE15': 'S', 'eE16': 'V', 'eE17': 'S', 'sn': {(1, 0): 'G', (1, 1): 'G', (2, 0): 'G', (3, 0): 'G', (3, 1): 'G'}, 'dEA': 14.263, 'SA': 76.977, 'qm': [(0, 0), (0, 1), (2, 0), (2, 1), (3, 0), (3, 1)], 'qbm': [0, 1, 2, 3], 'na': 4, 'nb': 4, 'iw': {(1, 1, 0): 'G', (2, 0, 0): 'G', (2, 0, 1): 'G', (2, 1, 0): 'S', (2, 1, 1): 'S', (3, 0, 0): 'G', (3, 0, 1): 'S', (3, 1, 0): 'S', (3, 1, 1): 'G'}, 'fused': [(0, 0), (0, 1)]}
 
 
 def tile_promp_trajectory_sampling_s7_kernel(tc, factor, noise_bytes, noise_scale, mean, basis, rnorm, amp, out):
@@ -55,7 +55,7 @@ def tile_promp_trajectory_sampling_s7_kernel(tc, factor, noise_bytes, noise_scal
         bas_v = basis.rearrange("(p n) b -> p n b", n=8)
         out_v = out.rearrange("(p n) j -> p n j", n=8)
 
-        nc.scalar.dma_start(out=nscale[:], in_=noise_scale.rearrange("(p t) o -> p (t o)", t=4))
+        nc.sync.dma_start(out=nscale[:], in_=noise_scale.rearrange("(p t) o -> p (t o)", t=4))
         nc.scalar.dma_start(out=mean_b[:], in_=mean.rearrange("(g p t) -> p g t", g=2, t=4))
         nc.scalar.dma_start(out=rn_b[:], in_=rnorm.rearrange("(p n) -> p n", n=8))
 
@@ -64,6 +64,9 @@ def tile_promp_trajectory_sampling_s7_kernel(tc, factor, noise_bytes, noise_scal
 
         def load_nz(c):
             nc.sync.dma_start(out=nz_bytes[:, c], in_=nz_v[c])
+
+        def load_amp(c0, c1):
+            nc.sync.dma_start(out=amp_b[:, CH * c0 : CH * c1], in_=amp[CH * c0 : CH * c1].partition_broadcast(P))
 
         def load_bas(n):
             nc.sync.dma_start(out=bas_rows[:, n : n + 2, :], in_=bas_v[:, n : n + 2, :])
@@ -79,9 +82,10 @@ def tile_promp_trajectory_sampling_s7_kernel(tc, factor, noise_bytes, noise_scal
         load_bas(2)
         load_nz(2)
         load_bas(4)
+        load_amp(0, 1)
         load_bas(6)
         load_nz(3)
-        nc.sync.dma_start(out=amp_b[:], in_=amp.partition_broadcast(P))
+        load_amp(1, 4)
 
         make_identity(nc, ident[:])
         nc.vector.memset(dummy[:], 0.0)
@@ -117,8 +121,8 @@ def tile_promp_trajectory_sampling_s7_kernel(tc, factor, noise_bytes, noise_scal
             o = bas_k[:, n].rearrange("p g r t -> p (g r t)").bitcast(F32)
             eng(out=o.rearrange("p (g r u) -> p g r u", g=2, u=2), in_=bank[:].rearrange("p (g u r) -> p g r u", g=2, u=2))
 
-        def quant_basis(n):
-            nc.vector.quantize_mx(out=bas_q[:, n].bitcast(FP8X4), scales=bas_s[:, n], in_=bas_k[:, n].rearrange("p g r i -> p (g r i)"))
+        def quant_basis(n0, n1):
+            nc.vector.quantize_mx(out=bas_q[:, n0:n1].rearrange("p n c -> p (n c)").bitcast(FP8X4), scales=bas_s[:, n0:n1].rearrange("p n c -> p (n c)"), in_=bas_k[:, n0:n1].rearrange("p n g r i -> p (n g r i)"))
 
 
         def A(name):
@@ -220,11 +224,11 @@ def tile_promp_trajectory_sampling_s7_kernel(tc, factor, noise_bytes, noise_scal
             cols = slice(HALF * h, HALF * (h + 1))
             interleave(e, w_tile(c, g)[:, cols, :], w_planes[c, g][:, :, cols])
 
-        def j_q(c, g, h):
+        def j_q(c, g, halves):
             if (c, g) not in w_q:
                 w_q[c, g] = stage.tile([P, CH], U32, name="w_q", align_bytes=64, bufs=6)
                 w_s[c, g] = stage.tile([P, CH], U8, name="w_s", align_bytes=64, bufs=6)
-            cols = slice(HALF * h, HALF * (h + 1))
+            cols = slice(HALF * halves[0], HALF * (halves[-1] + 1))
             nc.vector.quantize_mx(out=w_q[c, g][:, cols].bitcast(FP8X4), scales=w_s[c, g][:, cols], in_=w_woven[c, g][:, cols, :].rearrange("p n t -> p (n t)"))
 
         def j_s2(s):
@@ -253,10 +257,14 @@ def tile_promp_trajectory_sampling_s7_kernel(tc, factor, noise_bytes, noise_scal
             if e == "G":
                 nc.gpsimd.tensor_tensor(out=o, in0=half[s][:], in1=a, op=ALU.mult)
             else:
-                nc.vector.scalar_tensor_tensor(out=o, in0=bk["y", s][:], scalar=rn_f[:, n : n + 1], in1=a, op0=ALU.mult, op1=ALU.mult)
-            if s >= 30:
+                for x in range(2 if s == 31 else 1):
+                    w = slice(HALF * x, HALF * (x + 1)) if s == 31 else slice(0, CH)
+                    nc.vector.scalar_tensor_tensor(out=o[:, w], in0=bk["y", s][:, w], scalar=rn_f[:, n : n + 1], in1=a[:, w], op0=ALU.mult, op1=ALU.mult)
+                    if s == 31:
+                        nc.sync.dma_start(out=out_v[:, n, CH * c + HALF * x : CH * c + HALF * (x + 1)], in_=o[:, w])
+            if s == 30:
                 nc.sync.dma_start(out=out_v[:, n, CH * c : CH * (c + 1)], in_=o)
-            elif n % 2 == 1:
+            elif n % 2 == 1 and s != 31:
                 nc.sync.dma_start(out=out_v[:, n - 1 : n + 1, CH * c : CH * (c + 1)], in_=res[s // 2][:])
 
         for g in range(2):
@@ -267,7 +275,10 @@ def tile_promp_trajectory_sampling_s7_kernel(tc, factor, noise_bytes, noise_scal
         for n in range(8):
             at(A(f"Tb{n}"), ("Tb", n), [], j_tb, n)
             at(A(f"Eb{n}"), ("Eb", n), [("Tb", n)], j_eb, A(f"eEb{n}"), n)
-            at(A(f"qb{n}"), ("qb", n), [("Eb", n)], quant_basis, n)
+            if n // 2 not in A("qbm"):
+                at(A(f"qb{n}"), ("qb", n), [("Eb", n)], quant_basis, n, n + 1)
+            elif n % 2:
+                at(A(f"qb{n}"), ("qb", n), [("Eb", n - 1), ("Eb", n)], quant_basis, n - 1, n + 1)
         for c in range(NCH):
             for t in range(4):
                 at(A(f"wd{c}") + t * 0.01, ("wd", c, t), [], j_wd, A(f"ewd{c}"), c, t)
@@ -286,15 +297,19 @@ def tile_promp_trajectory_sampling_s7_kernel(tc, factor, noise_bytes, noise_scal
             for i in range(4):
                 g, h = divmod(i, 2)
                 k = A(f"I0{i}") if c == 0 else 8 * c - A(f"AI{c}") + i * A(f"rI{c}")
-                e1 = [("E1", c, g, t) for t in range(4)]
-                if (c, g) in A("fused"):
-                    at(A(f"Q0{i}") if c == 0 else k + A("dQ"), ("Q", c, g, h), [("E1", c, g, 2 * h), ("E1", c, g, 2 * h + 1)], j_q, c, g, h)
-                else:
-                    at(k, ("I", c, g, h), e1, j_i, A("iw").get((c, g, h), "V"), c, g, h)
-                    at(A(f"Q0{i}") if c == 0 else k + A("dQ"), ("Q", c, g, h), [("I", c, g, h)], j_q, c, g, h)
+                fused = (c, g) in A("fused")
+                if not fused:
+                    at(k, ("I", c, g, h), [("E1", c, g, t) for t in range(4)], j_i, A("iw").get((c, g, h), "V"), c, g, h)
+                kq = A(f"Q0{i}") if c == 0 else k + A("dQ")
+                whole = (c, g) in A("qm")
+                if whole and h == 0:
+                    continue
+                halves = (0, 1) if whole else (h,)
+                src = [("E1", c, g, 2 * x + y) for x in halves for y in range(2)] if fused else [("I", c, g, x) for x in halves]
+                at(kq, ("Q", c, g, h), src, j_q, c, g, halves)
         for s in range(8 * NCH):
             c, n = divmod(s, 8)
-            at(s, ("S2", s), [("qb", n)] + [("Q", c, g, h) for g in range(2) for h in range(2)], j_s2, s)
+            at(s, ("S2", s), [("qb", n | 1 if n // 2 in A("qbm") else n)] + [("Q", c, g, h) for g in range(2) for h in range(2) if h or (c, g) not in A("qm")], j_s2, s)
             if s in A("epg"):
                 at(s + A("dF"), ("Y", s), [("S2", s)], j_y, s)
                 at(s + A("dF"), ("F", s), [("Y", s)], j_f, "G", s)

@@ -12,312 +12,359 @@ U32 = mybir.dt.uint32
 U8 = mybir.dt.uint8
 FP8 = mybir.dt.float8_e4m3fn
 FP8X4 = mybir.dt.float8_e4m3fn_x4
-ALU = mybir.AluOpType
-ACT = mybir.ActivationFunctionType
+ADD = mybir.AluOpType.add
+MULT = mybir.AluOpType.mult
+COPY = mybir.ActivationFunctionType.Copy
+IDENTITY = mybir.ActivationFunctionType.Identity
 
 P = 128
-CH = 512
-NCH = N // CH
-HALF = 256
-PLAN = {'epg': [], 'inh': -86.539, 'dQ': -14.564, 'dF': -14.488, 'dE': -121.021, 'S10': -91.812, 'rS10': 3.092, 'Tf00': -196.155, 'Ef00': -164.646, 'eEf00': 'S', 'Tf01': -130.886, 'Ef01': -142.394, 'eEf01': 'S', 'Tf10': -129.331, 'Ef10': -118.99, 'eEf10': 'S', 'Tf11': -117.046, 'Ef11': -137.297, 'eEf11': 'V', 'qf0': -140.053, 'qf1': -149.502, 'wd0': -165.235, 'in0': -302.469, 'qn0': -130.987, 'ewd0': 'V', 'wd1': -49.887, 'in1': -276.174, 'qn1': -131.883, 'ewd1': 'S', 'wd2': -37.534, 'in2': -39.696, 'qn2': -11.086, 'ewd2': 'S', 'wd3': 4.297, 'in3': 10.997, 'qn3': -41.618, 'ewd3': 'S', 'A11': 13.941, 'r11': 1.242, 'AI1': 69.313, 'rI1': -98.495, 'A12': 13.083, 'r12': 0.779, 'AI2': 2.465, 'rI2': -0.201, 'A13': 9.781, 'r13': 0.286, 'AI3': 3.077, 'rI3': 0.313, 'I00': -110.556, 'Q00': -134.424, 'I01': 148.869, 'Q01': -25.98, 'I02': 10.641, 'Q02': -98.864, 'I03': -238.389, 'Q03': -231.086, 'Tb0': -12.674, 'Eb0': -60.812, 'qb0': -85.051, 'eEb0': 'S', 'Tb1': -10.849, 'Eb1': -175.241, 'qb1': -40.442, 'eEb1': 'S', 'Tb2': -10.483, 'Eb2': -49.954, 'qb2': -192.993, 'eEb2': 'S', 'Tb3': -34.225, 'Eb3': -68.496, 'qb3': -29.812, 'eEb3': 'S', 'Tb4': -15.149, 'Eb4': -58.666, 'qb4': -116.279, 'eEb4': 'S', 'Tb5': -30.034, 'Eb5': -74.803, 'qb5': -2.497, 'eEb5': 'S', 'Tb6': -7.4, 'Eb6': -201.352, 'qb6': -106.916, 'eEb6': 'S', 'Tb7': -8.654, 'Eb7': -118.854, 'qb7': -186.722, 'eEb7': 'S', 'eE10': 'S', 'eE11': 'V', 'eE12': 'S', 'eE13': 'V', 'eE14': 'S', 'eE15': 'S', 'eE16': 'V', 'eE17': 'S', 'sn': {(1, 0): 'G', (1, 1): 'G', (2, 0): 'G', (3, 0): 'G', (3, 1): 'G'}, 'dEA': 14.263, 'SA': 76.977, 'qm': [(0, 0), (0, 1), (2, 0), (2, 1), (3, 0), (3, 1)], 'qbm': [0, 1, 2, 3], 'na': 4, 'nb': 4, 'iw': {(1, 1, 0): 'G', (2, 0, 0): 'G', (2, 0, 1): 'G', (2, 1, 0): 'S', (2, 1, 1): 'S', (3, 0, 0): 'G', (3, 0, 1): 'S', (3, 1, 0): 'S', (3, 1, 1): 'G'}, 'fused': [(0, 0), (0, 1)]}
+PACK = 4
+PASSES = B // (P * PACK)
+CHUNK = 512
+HALF = CHUNK // 2
+CHUNKS = N // CHUNK
+TILES = T // P
+LAST = CHUNKS * TILES - 1
+
+FIRST_ISSUED = (5, 6, 7, 9, 10, 11, 13, 14, 15, 16, 16, 16, 16, 16, 16, 19, 23, 24)
 
 
-def tile_promp_trajectory_sampling_s7_kernel(tc, factor, noise_bytes, noise_scale, mean, basis, rnorm, amp, out):
+def tile_promp_trajectory_sampling_s7_kernel(
+    tc, factor, noise_bytes, noise_scale, mean, basis, rnorm, amp, out
+):
     nc = tc.nc
     with ExitStack() as ctx:
         keep = ctx.enter_context(tc.tile_pool(name="keep", bufs=1))
-        stage = ctx.enter_context(tc.tile_pool(name="stage", bufs=2))
-        psum = ctx.enter_context(tc.psum_pool(name="psum", bufs=PLAN["na"]))
-        psum2 = ctx.enter_context(tc.psum_pool(name="psum2", bufs=PLAN["nb"]))
+        stage = ctx.enter_context(tc.tile_pool(name="stage", bufs=3))
+        psum_first = ctx.enter_context(tc.psum_pool(name="psum_first", bufs=4))
+        psum_second = ctx.enter_context(tc.psum_pool(name="psum_second", bufs=4))
 
-        ident = keep.tile([P, P], F32, name="ident")
-        dummy = keep.tile([P, 1], F32, name="dummy")
-        nscale = keep.tile([P, 4], F32, name="nscale")
-        mean_b = keep.tile([P, 2, 4], BF16, name="mean_b")
-        mean_f = keep.tile([P, 2, 4], F32, name="mean_f")
-        rn_b = keep.tile([P, 8], BF16, name="rn_b")
-        rn_f = keep.tile([P, 8], F32, name="rn_f")
-        amp_b = keep.tile([P, N], BF16, name="amp_b")
-        fac_rows = keep.tile([P, 2, 4, R], BF16, name="fac_rows")
-        fac_k = keep.tile([P, 2, 4, P, 4], BF16, name="fac_k", align_bytes=64)
-        fac_q = keep.tile([P, 2, 4 * P], U32, name="fac_q", align_bytes=64)
-        fac_s = keep.tile([P, 2, 4 * P], U8, name="fac_s", align_bytes=64)
-        bas_rows = keep.tile([P, 8, B], BF16, name="bas_rows")
-        bas_k = keep.tile([P, 8, 2, P, 4], BF16, name="bas_k", align_bytes=64)
-        bas_q = keep.tile([P, 8, 2 * P], U32, name="bas_q", align_bytes=64)
-        bas_s = keep.tile([P, 8, 2 * P], U8, name="bas_s", align_bytes=64)
-        nz_bytes = keep.tile([P, NCH, 4, CH], U8, name="nz_bytes")
-        nz_q = keep.tile([P, NCH, CH], U32, name="nz_q", align_bytes=64)
-        nz_s = keep.tile([P, NCH, CH], U8, name="nz_s", align_bytes=64)
+        factor_rows = keep.tile([P, PASSES, PACK, R], BF16, name="factor_rows")
+        factor_woven = keep.tile([P, PASSES, PACK, P, PACK], BF16, name="factor_woven", align_bytes=64)
+        factor_codes = keep.tile([P, PASSES, PACK * P], U32, name="factor_codes", align_bytes=64)
+        factor_scales = keep.tile([P, PASSES, PACK * P], U8, name="factor_scales", align_bytes=64)
+        basis_rows = keep.tile([P, TILES, B], BF16, name="basis_rows")
+        basis_woven = keep.tile([P, TILES, PASSES, P, PACK], BF16, name="basis_woven", align_bytes=64)
+        basis_codes = keep.tile([P, TILES, PASSES * P], U32, name="basis_codes", align_bytes=64)
+        basis_scales = keep.tile([P, TILES, PASSES * P], U8, name="basis_scales", align_bytes=64)
+        noise_codes_in = keep.tile([P, CHUNKS, PACK, CHUNK], U8, name="noise_codes_in")
+        noise_codes = keep.tile([P, CHUNKS, CHUNK], U32, name="noise_codes", align_bytes=64)
+        noise_scales = keep.tile([P, CHUNKS, CHUNK], U8, name="noise_scales", align_bytes=64)
+        byte_scale = keep.tile([P, PACK], F32, name="byte_scale")
+        mean_in = keep.tile([P, PASSES, PACK], BF16, name="mean_in")
+        mean_f32 = keep.tile([P, PASSES, PACK], F32, name="mean_f32")
+        rnorm_in = keep.tile([P, TILES], BF16, name="rnorm_in")
+        rnorm_f32 = keep.tile([P, TILES], F32, name="rnorm_f32")
+        amp_all = keep.tile([P, N], BF16, name="amp_all")
+        identity = keep.tile([P, P], F32, name="identity")
+        warm = keep.tile([P, 1], F32, name="warm")
 
-        fac_v = factor.rearrange("(g m t) k -> g m t k", g=2, t=4)
-        nz_v = noise_bytes.rearrange("(p t) (c n) -> c p t n", t=4, n=CH)
-        bas_v = basis.rearrange("(p n) b -> p n b", n=8)
-        out_v = out.rearrange("(p n) j -> p n j", n=8)
+        factor_hbm = factor.rearrange("(g m t) r -> g m t r", g=PASSES, t=PACK)
+        noise_hbm = noise_bytes.rearrange("(p t) (c j) -> c p t j", t=PACK, j=CHUNK)
+        basis_hbm = basis.rearrange("(p n) b -> p n b", n=TILES)
+        out_hbm = out.rearrange("(p n) j -> p n j", n=TILES)
 
-        nc.sync.dma_start(out=nscale[:], in_=noise_scale.rearrange("(p t) o -> p (t o)", t=4))
-        nc.scalar.dma_start(out=mean_b[:], in_=mean.rearrange("(g p t) -> p g t", g=2, t=4))
-        nc.scalar.dma_start(out=rn_b[:], in_=rnorm.rearrange("(p n) -> p n", n=8))
+        def load_factor(g, a):
+            slots = slice(2 * a, 2 * a + 2)
+            nc.sync.dma_start(out=factor_rows[:, g, slots, :], in_=factor_hbm[g][:, slots, :])
 
-        def load_fac(g, h):
-            nc.sync.dma_start(out=fac_rows[:, g, 2 * h : 2 * h + 2, :], in_=fac_v[g][:, 2 * h : 2 * h + 2, :])
+        def load_noise(c):
+            nc.sync.dma_start(out=noise_codes_in[:, c], in_=noise_hbm[c])
 
-        def load_nz(c):
-            nc.sync.dma_start(out=nz_bytes[:, c], in_=nz_v[c])
+        def load_basis(n):
+            nc.sync.dma_start(out=basis_rows[:, n : n + 2, :], in_=basis_hbm[:, n : n + 2, :])
 
-        def load_amp(c0, c1):
-            nc.sync.dma_start(out=amp_b[:, CH * c0 : CH * c1], in_=amp[CH * c0 : CH * c1].partition_broadcast(P))
+        def load_amp(first, end):
+            cols = slice(CHUNK * first, CHUNK * end)
+            nc.sync.dma_start(out=amp_all[:, cols], in_=amp[cols].partition_broadcast(P))
 
-        def load_bas(n):
-            nc.sync.dma_start(out=bas_rows[:, n : n + 2, :], in_=bas_v[:, n : n + 2, :])
-
-        for h in range(2):
-            nc.sync.dma_start(out=nz_bytes[:, 0, 2 * h : 2 * h + 2], in_=nz_v[0][:, 2 * h : 2 * h + 2])
-        load_fac(0, 0)
-        load_fac(0, 1)
-        load_fac(1, 0)
-        load_fac(1, 1)
-        load_bas(0)
-        load_nz(1)
-        load_bas(2)
-        load_nz(2)
-        load_bas(4)
-        load_amp(0, 1)
-        load_bas(6)
-        load_nz(3)
-        load_amp(1, 4)
-
-        make_identity(nc, ident[:])
-        nc.vector.memset(dummy[:], 0.0)
-        nc.scalar.activation(out=dummy[:], in_=dummy[:], func=ACT.Identity)
-
-        fac_w = fac_rows[:].bitcast(F32)
-        bas_w = bas_rows[:].bitcast(F32)
-
-        def turn_factor(g, h):
-            bank = psum.tile([P, CH], F32, name="bank")
+        nc.sync.dma_start(out=byte_scale[:], in_=noise_scale.rearrange("(p t) o -> p (t o)", t=PACK))
+        nc.scalar.dma_start(out=mean_in[:], in_=mean.rearrange("(g p t) -> p g t", g=PASSES, t=PACK))
+        nc.scalar.dma_start(out=rnorm_in[:], in_=rnorm.rearrange("(p n) -> p n", n=TILES))
+        for t in (0, 2):
+            nc.sync.dma_start(out=noise_codes_in[:, 0, t : t + 2], in_=noise_hbm[0][:, t : t + 2])
+        for g in range(PASSES):
             for a in range(2):
+                load_factor(g, a)
+        load_basis(0)
+        load_noise(1)
+        load_basis(2)
+        load_noise(2)
+        load_basis(4)
+        load_amp(0, 1)
+        load_basis(6)
+        load_noise(3)
+        load_amp(1, CHUNKS)
+
+        make_identity(nc, identity[:])
+        nc.vector.memset(warm[:], 0.0)
+        nc.scalar.activation(out=warm[:], in_=warm[:], func=IDENTITY)
+
+        factor_words = factor_rows[:].bitcast(F32)
+        basis_words = basis_rows[:].bitcast(F32)
+
+        def turn_factor(g, a):
+            bank = psum_first.tile([P, 2, 2, P], F32, name="bank_first")
+            for x in range(2):
                 for u in range(2):
-                    nc.tensor.transpose(bank[:, P * (2 * a + u) : P * (2 * a + u + 1)], fac_w[:, g, 2 * h + a, u::2], ident[:])
+                    nc.tensor.transpose(bank[:, x, u, :], factor_words[:, g, 2 * a + x, u::2], identity[:])
             return bank
 
-        def empty_factor(e, bank, g, h):
-            eng = nc.scalar.copy if e == 'S' else nc.vector.tensor_copy
-            o = fac_k[:, g, 2 * h : 2 * h + 2].rearrange("p a r t -> p (a r t)").bitcast(F32)
-            eng(out=o.rearrange("p (a r u) -> p a r u", a=2, u=2), in_=bank[:].rearrange("p (a u r) -> p a r u", a=2, u=2))
+        def empty_factor(copy, bank, g, a):
+            woven = factor_woven[:, g, 2 * a : 2 * a + 2].rearrange("p x m t -> p (x m t)").bitcast(F32)
+            copy(
+                out=woven.rearrange("p (x m u) -> p x m u", x=2, u=2),
+                in_=bank[:].rearrange("p x u m -> p x m u"),
+            )
 
-        def quant_factor(g):
-            nc.vector.quantize_mx(out=fac_q[:, g].bitcast(FP8X4), scales=fac_s[:, g], in_=fac_k[:, g].rearrange("p t r i -> p (t r i)"))
+        def quantize_factor(g):
+            nc.vector.quantize_mx(
+                out=factor_codes[:, g].bitcast(FP8X4),
+                scales=factor_scales[:, g],
+                in_=factor_woven[:, g].rearrange("p t m k -> p (t m k)"),
+            )
 
         def turn_basis(n):
-            bank = psum.tile([P, CH], F32, name="bank")
-            for g in range(2):
+            bank = psum_second.tile([P, PASSES, 2, P], F32, name="bank_second")
+            for g in range(PASSES):
+                first = P * 2 * g
                 for u in range(2):
-                    nc.tensor.transpose(bank[:, P * (2 * g + u) : P * (2 * g + u + 1)], bas_w[:, n, 256 * g + u : 256 * (g + 1) : 2], ident[:])
+                    words = slice(first + u, first + P * 2, 2)
+                    nc.tensor.transpose(bank[:, g, u, :], basis_words[:, n, words], identity[:])
             return bank
 
-        def empty_basis(e, bank, n):
-            eng = nc.scalar.copy if e == 'S' else nc.vector.tensor_copy
-            o = bas_k[:, n].rearrange("p g r t -> p (g r t)").bitcast(F32)
-            eng(out=o.rearrange("p (g r u) -> p g r u", g=2, u=2), in_=bank[:].rearrange("p (g u r) -> p g r u", g=2, u=2))
+        def empty_basis(bank, n):
+            woven = basis_woven[:, n].rearrange("p g m t -> p (g m t)").bitcast(F32)
+            nc.scalar.copy(
+                out=woven.rearrange("p (g m u) -> p g m u", g=PASSES, u=2),
+                in_=bank[:].rearrange("p g u m -> p g m u"),
+            )
 
-        def quant_basis(n0, n1):
-            nc.vector.quantize_mx(out=bas_q[:, n0:n1].rearrange("p n c -> p (n c)").bitcast(FP8X4), scales=bas_s[:, n0:n1].rearrange("p n c -> p (n c)"), in_=bas_k[:, n0:n1].rearrange("p n g r i -> p (n g r i)"))
+        def quantize_basis(n):
+            pair = slice(n, n + 2)
+            nc.vector.quantize_mx(
+                out=basis_codes[:, pair].rearrange("p n k -> p (n k)").bitcast(FP8X4),
+                scales=basis_scales[:, pair].rearrange("p n k -> p (n k)"),
+                in_=basis_woven[:, pair].rearrange("p n g m t -> p (n g m t)"),
+            )
 
+        def weave(engine, woven, planes, half):
+            cols = slice(HALF * half, HALF * (half + 1))
+            dst = woven[:, cols, :]
+            src = planes[:, :, cols]
+            if engine == "gpsimd":
+                nc.gpsimd.tensor_scalar(
+                    out=dst, in0=src.rearrange("p t j -> p j t"), scalar1=1.0, scalar2=0.0, op0=MULT, op1=ADD
+                )
+                return
+            copy = nc.scalar.copy if engine == "scalar" else nc.vector.tensor_copy
+            copy(
+                out=dst.rearrange("p (j i) t -> p j t i", i=4),
+                in_=src.rearrange("p t (j i) -> p j t i", i=4),
+            )
 
-        def A(name):
-            return PLAN[name]
+        noise_planes = {}
+        noise_woven = {}
 
-        work = []
-        keys = {}
+        def widen_noise(engine, c):
+            noise_planes[c] = stage.tile([P, PACK, CHUNK], BF16, name="noise_planes")
+            noise_woven[c] = stage.tile([P, CHUNK, PACK], BF16, name="noise_woven", align_bytes=64)
+            for t in range(PACK):
+                src = noise_codes_in[:, c, t, :].bitcast(FP8)
+                dst = noise_planes[c][:, t, :]
+                scale = byte_scale[:, t : t + 1]
+                if engine == "scalar":
+                    nc.scalar.activation(out=dst, in_=src, func=COPY, scale=scale)
+                else:
+                    nc.vector.tensor_scalar(out=dst, in0=src, scalar1=scale, scalar2=None, op0=MULT)
 
-        def at(step, name, deps, job, *args):
-            step = max([step] + [keys[d] + 0.0001 for d in deps])
-            keys[name] = step
-            work.append((step, len(work), job, args))
+        def weave_noise(engine, c, half):
+            weave(engine, noise_woven[c], noise_planes[c], half)
 
-        bk = {}
-        planes = {}
-        woven = {}
+        def quantize_noise(c):
+            nc.vector.quantize_mx(
+                out=noise_codes[:, c].bitcast(FP8X4),
+                scales=noise_scales[:, c],
+                in_=noise_woven[c][:].rearrange("p j t -> p (j t)"),
+            )
+
         w_planes = {}
         w_woven = {}
-        w_q = {}
-        w_s = {}
-        res = {}
-        half = {}
+        w_codes = {}
+        w_scales = {}
 
-        def j_tf(g, h):
-            bk["f", g, h] = turn_factor(g, h)
+        def first_pass(bank, g, t, c, cols):
+            rows = slice(P * t, P * (t + 1))
+            nc.tensor.matmul_mx(
+                out=bank,
+                lhsT=factor_codes[:, g, rows].bitcast(FP8X4),
+                lhsT_scale=factor_scales[:, g, rows],
+                rhs=noise_codes[:, c, cols].bitcast(FP8X4),
+                rhs_scale=noise_scales[:, c, cols],
+                start=True,
+                stop=True,
+            )
 
-        def j_ef(e, g, h):
-            empty_factor(e, bk["f", g, h], g, h)
+        def w_tiles(c, g):
+            w_woven[c, g] = stage.tile([P, CHUNK, PACK], BF16, name="w_woven", align_bytes=64, bufs=4)
+            w_codes[c, g] = stage.tile([P, CHUNK], U32, name="w_codes", align_bytes=64, bufs=6)
+            w_scales[c, g] = stage.tile([P, CHUNK], U8, name="w_scales", align_bytes=64, bufs=6)
 
-        def j_tb(n):
-            bk["b", n] = turn_basis(n)
+        def first_woven(g, quarter):
+            bank = psum_first.tile([P, PACK, P], F32, name="bank_first")
+            cols = slice(P * quarter, P * (quarter + 1))
+            for t in range(PACK):
+                first_pass(bank[:, t, :], g, t, 0, cols)
+            return bank
 
-        def j_eb(e, n):
-            empty_basis(e, bk["b", n], n)
+        def empty_woven(bank, g, quarter):
+            nc.vector.tensor_tensor(
+                out=w_woven[0, g][:, P * quarter : P * (quarter + 1), :],
+                in0=bank[:].rearrange("p t j -> p j t"),
+                in1=mean_f32[:, g, :].unsqueeze(1).to_broadcast([P, P, PACK]),
+                op=ADD,
+            )
 
-        def j_wd(e, c, t):
-            if c not in planes:
-                planes[c] = stage.tile([P, 4, CH], BF16, name="nz_planes", bufs=3)
-            src = nz_bytes[:, c, t, :].bitcast(FP8)
-            if e == "S":
-                nc.scalar.activation(out=planes[c][:, t, :], in_=src, func=ACT.Copy, scale=nscale[:, t : t + 1])
-            else:
-                nc.vector.tensor_scalar(out=planes[c][:, t, :], in0=src, scalar1=nscale[:, t : t + 1], scalar2=None, op0=ALU.mult)
+        def first_plane(c, g, t):
+            if t == 0:
+                w_tiles(c, g)
+                w_planes[c, g] = stage.tile([P, PACK, CHUNK], BF16, name="w_planes", bufs=4)
+            bank = psum_first.tile([P, CHUNK], F32, name="bank_first")
+            first_pass(bank[:], g, t, c, slice(0, CHUNK))
+            nc.scalar.activation(
+                out=w_planes[c, g][:, t, :], in_=bank[:], func=IDENTITY, bias=mean_f32[:, g, t : t + 1]
+            )
 
-        def interleave(e, dst, src):
-            d = dst.rearrange("p (c i) t -> p c t i", i=4)
-            s = src.rearrange("p t (c i) -> p c t i", i=4)
-            if e == "S":
-                nc.scalar.copy(out=d, in_=s)
-            elif e == "G":
-                nc.gpsimd.tensor_scalar(out=dst, in0=src.rearrange("p t n -> p n t"), scalar1=1.0, scalar2=0.0, op0=ALU.mult, op1=ALU.add)
-            else:
-                nc.vector.tensor_copy(out=d, in_=s)
+        def weave_w(engine, c, g, half):
+            weave(engine, w_woven[c, g], w_planes[c, g], half)
 
-        def j_in(e, c, h):
-            if c not in woven:
-                woven[c] = stage.tile([P, CH, 4], BF16, name="nz_woven", align_bytes=64, bufs=3)
-            cols = slice(HALF * h, HALF * (h + 1))
-            interleave(e, woven[c][:, cols, :], planes[c][:, :, cols])
+        def quantize_w(c, g, cols):
+            nc.vector.quantize_mx(
+                out=w_codes[c, g][:, cols].bitcast(FP8X4),
+                scales=w_scales[c, g][:, cols],
+                in_=w_woven[c, g][:, cols, :].rearrange("p j t -> p (j t)"),
+            )
 
-        def j_qn(c):
-            nc.vector.quantize_mx(out=nz_q[:, c].bitcast(FP8X4), scales=nz_s[:, c], in_=woven[c][:].rearrange("p n t -> p (n t)"))
+        whole = slice(0, CHUNK)
+        halves = (slice(0, HALF), slice(HALF, CHUNK))
 
-        def j_s1(c, g, t):
-            bank = psum.tile([P, CH], F32, name="bank")
-            bk["w", c, g, t] = bank
-            nc.tensor.matmul_mx(out=bank[:], lhsT=fac_q[:, g, P * t : P * (t + 1)].bitcast(FP8X4), lhsT_scale=fac_s[:, g, P * t : P * (t + 1)],
-                                rhs=nz_q[:, c].bitcast(FP8X4), rhs_scale=nz_s[:, c], start=True, stop=True)
+        results = {}
 
-        def j_e1(e, c, g, t):
-            if (c, g) not in w_planes:
-                w_planes[c, g] = stage.tile([P, 4, CH], BF16, name="w_planes", bufs=4)
-            o = w_planes[c, g][:, t, :]
-            b = bk["w", c, g, t]
-            if e == "S":
-                nc.scalar.activation(out=o, in_=b[:], func=ACT.Identity, bias=mean_f[:, g, t : t + 1])
-            else:
-                nc.vector.tensor_scalar(out=o, in0=b[:], scalar1=mean_f[:, g, t : t + 1], scalar2=None, op0=ALU.add)
+        def second_tile(s):
+            c, n = divmod(s, TILES)
+            bank = psum_second.tile([P, CHUNK], F32, name="bank_second")
+            for g in range(PASSES):
+                phases = slice(P * g, P * (g + 1))
+                nc.tensor.matmul_mx(
+                    out=bank[:],
+                    lhsT=basis_codes[:, n, phases].bitcast(FP8X4),
+                    lhsT_scale=basis_scales[:, n, phases],
+                    rhs=w_codes[c, g][:].bitcast(FP8X4),
+                    rhs_scale=w_scales[c, g][:],
+                    start=(g == 0),
+                    stop=(g == PASSES - 1),
+                )
+            return bank
 
-        def j_s1f(c, g, blk):
-            bank = psum.tile([P, CH], F32, name="bank")
-            bk["w", c, g, blk] = bank
-            cols = slice(P * blk, P * (blk + 1))
-            for t in range(4):
-                nc.tensor.matmul_mx(out=bank[:, P * t : P * (t + 1)], lhsT=fac_q[:, g, P * t : P * (t + 1)].bitcast(FP8X4), lhsT_scale=fac_s[:, g, P * t : P * (t + 1)],
-                                    rhs=nz_q[:, c, cols].bitcast(FP8X4), rhs_scale=nz_s[:, c, cols], start=True, stop=True)
-
-        def j_e1f(c, g, blk):
-            o = w_tile(c, g)[:, P * blk : P * (blk + 1), :]
-            m = mean_f[:, g, :].unsqueeze(1).to_broadcast([P, P, 4])
-            nc.vector.tensor_tensor(out=o, in0=bk["w", c, g, blk][:].rearrange("p (t n) -> p n t", t=4), in1=m, op=ALU.add)
-
-        def w_tile(c, g):
-            if (c, g) not in w_woven:
-                w_woven[c, g] = stage.tile([P, CH, 4], BF16, name="w_woven", align_bytes=64, bufs=4)
-            return w_woven[c, g]
-
-        def j_i(e, c, g, h):
-            cols = slice(HALF * h, HALF * (h + 1))
-            interleave(e, w_tile(c, g)[:, cols, :], w_planes[c, g][:, :, cols])
-
-        def j_q(c, g, halves):
-            if (c, g) not in w_q:
-                w_q[c, g] = stage.tile([P, CH], U32, name="w_q", align_bytes=64, bufs=6)
-                w_s[c, g] = stage.tile([P, CH], U8, name="w_s", align_bytes=64, bufs=6)
-            cols = slice(HALF * halves[0], HALF * (halves[-1] + 1))
-            nc.vector.quantize_mx(out=w_q[c, g][:, cols].bitcast(FP8X4), scales=w_s[c, g][:, cols], in_=w_woven[c, g][:, cols, :].rearrange("p n t -> p (n t)"))
-
-        def j_s2(s):
-            c, n = divmod(s, 8)
-            if s >= A("SA") and s % 2:
-                bank = psum.tile([P, CH], F32, name="bank")
-            else:
-                bank = psum2.tile([P, CH], F32, name="sum")
-            bk["y", s] = bank
-            for g in range(2):
-                cols = slice(P * g, P * (g + 1))
-                nc.tensor.matmul_mx(out=bank[:], lhsT=bas_q[:, n, cols].bitcast(FP8X4), lhsT_scale=bas_s[:, n, cols],
-                                    rhs=w_q[c, g][:].bitcast(FP8X4), rhs_scale=w_s[c, g][:], start=(g == 0), stop=(g == 1))
-
-        def j_y(s):
-            n = s % 8
-            half[s] = stage.tile([P, CH], F32, name="half_done", bufs=3)
-            nc.scalar.activation(out=half[s][:], in_=bk["y", s][:], func=ACT.Copy, scale=rn_f[:, n : n + 1])
-
-        def j_f(e, s):
-            c, n = divmod(s, 8)
-            if s // 2 not in res:
-                res[s // 2] = stage.tile([P, 2, CH], F32, name="res", bufs=5)
-            o = res[s // 2][:, n % 2, :]
-            a = amp_b[:, CH * c : CH * (c + 1)]
-            if e == "G":
-                nc.gpsimd.tensor_tensor(out=o, in0=half[s][:], in1=a, op=ALU.mult)
-            else:
-                for x in range(2 if s == 31 else 1):
-                    w = slice(HALF * x, HALF * (x + 1)) if s == 31 else slice(0, CH)
-                    nc.vector.scalar_tensor_tensor(out=o[:, w], in0=bk["y", s][:, w], scalar=rn_f[:, n : n + 1], in1=a[:, w], op0=ALU.mult, op1=ALU.mult)
-                    if s == 31:
-                        nc.sync.dma_start(out=out_v[:, n, CH * c + HALF * x : CH * c + HALF * (x + 1)], in_=o[:, w])
-            if s == 30:
-                nc.sync.dma_start(out=out_v[:, n, CH * c : CH * (c + 1)], in_=o)
-            elif n % 2 == 1 and s != 31:
-                nc.sync.dma_start(out=out_v[:, n - 1 : n + 1, CH * c : CH * (c + 1)], in_=res[s // 2][:])
-
-        for g in range(2):
-            for h in range(2):
-                at(A(f"Tf{g}{h}"), ("Tf", g, h), [], j_tf, g, h)
-                at(A(f"Ef{g}{h}"), ("Ef", g, h), [("Tf", g, h)], j_ef, A(f"eEf{g}{h}"), g, h)
-            at(A(f"qf{g}"), ("qf", g), [("Ef", g, 0), ("Ef", g, 1)], quant_factor, g)
-        for n in range(8):
-            at(A(f"Tb{n}"), ("Tb", n), [], j_tb, n)
-            at(A(f"Eb{n}"), ("Eb", n), [("Tb", n)], j_eb, A(f"eEb{n}"), n)
-            if n // 2 not in A("qbm"):
-                at(A(f"qb{n}"), ("qb", n), [("Eb", n)], quant_basis, n, n + 1)
-            elif n % 2:
-                at(A(f"qb{n}"), ("qb", n), [("Eb", n - 1), ("Eb", n)], quant_basis, n - 1, n + 1)
-        for c in range(NCH):
-            for t in range(4):
-                at(A(f"wd{c}") + t * 0.01, ("wd", c, t), [], j_wd, A(f"ewd{c}"), c, t)
-            for h in range(2):
-                at(A(f"in{c}") + h * A("inh"), ("in", c, h), [("wd", c, t) for t in range(4)], j_in, A("sn").get((c, h), "V"), c, h)
-            at(A(f"qn{c}"), ("qn", c), [("in", c, 0), ("in", c, 1)], j_qn, c)
-            for u in range(8):
-                g, t = divmod(u, 4)
-                k = A("S10") + u * A("rS10") if c == 0 else 8 * c - A(f"A1{c}") + u * A(f"r1{c}")
-                if (c, g) in A("fused"):
-                    at(k, ("S1", c, g, t), [("qn", c), ("qf", g)], j_s1f, c, g, t)
-                    at(k + A("dEA"), ("E1", c, g, t), [("S1", c, g, t)], j_e1f, c, g, t)
-                    continue
-                at(k, ("S1", c, g, t), [("qn", c), ("qf", g)], j_s1, c, g, t)
-                at(k + A("dE"), ("E1", c, g, t), [("S1", c, g, t)], j_e1, A(f"eE1{u}") if c == 0 else "S", c, g, t)
-            for i in range(4):
-                g, h = divmod(i, 2)
-                k = A(f"I0{i}") if c == 0 else 8 * c - A(f"AI{c}") + i * A(f"rI{c}")
-                fused = (c, g) in A("fused")
-                if not fused:
-                    at(k, ("I", c, g, h), [("E1", c, g, t) for t in range(4)], j_i, A("iw").get((c, g, h), "V"), c, g, h)
-                kq = A(f"Q0{i}") if c == 0 else k + A("dQ")
-                whole = (c, g) in A("qm")
-                if whole and h == 0:
-                    continue
-                halves = (0, 1) if whole else (h,)
-                src = [("E1", c, g, 2 * x + y) for x in halves for y in range(2)] if fused else [("I", c, g, x) for x in halves]
-                at(kq, ("Q", c, g, h), src, j_q, c, g, halves)
-        for s in range(8 * NCH):
-            c, n = divmod(s, 8)
-            at(s, ("S2", s), [("qb", n | 1 if n // 2 in A("qbm") else n)] + [("Q", c, g, h) for g in range(2) for h in range(2) if h or (c, g) not in A("qm")], j_s2, s)
-            if s in A("epg"):
-                at(s + A("dF"), ("Y", s), [("S2", s)], j_y, s)
-                at(s + A("dF"), ("F", s), [("Y", s)], j_f, "G", s)
-            else:
-                at(s + A("dF"), ("F", s), [("S2", s)], j_f, "V", s)
+        def finish_tile(s, bank):
+            c, n = divmod(s, TILES)
+            if n % 2 == 0:
+                results[s // 2] = stage.tile([P, 2, CHUNK], F32, name="result", bufs=5)
+            result = results[s // 2]
+            for cols in halves if s == LAST else (whole,):
+                out_cols = slice(CHUNK * c + cols.start, CHUNK * c + cols.stop)
+                nc.vector.scalar_tensor_tensor(
+                    out=result[:, n % 2, cols],
+                    in0=bank[:, cols],
+                    scalar=rnorm_f32[:, n : n + 1],
+                    in1=amp_all[:, out_cols],
+                    op0=MULT,
+                    op1=MULT,
+                )
+                if s >= LAST - 1:
+                    nc.sync.dma_start(out=out_hbm[:, n, out_cols], in_=result[:, n % 2, cols])
+            if n % 2 == 1 and s != LAST:
+                nc.sync.dma_start(out=out_hbm[:, n - 1 : n + 1, CHUNK * c : CHUNK * (c + 1)], in_=result[:])
 
         with tc.manual_schedule():
-            nc.vector.tensor_copy(out=mean_f[:], in_=mean_b[:])
-            nc.vector.tensor_copy(out=rn_f[:], in_=rn_b[:])
-            for step, order, job, args in sorted(work, key=lambda w: w[:2]):
-                job(*args)
+            nc.vector.tensor_copy(out=mean_f32[:], in_=mean_in[:])
+            nc.vector.tensor_copy(out=rnorm_f32[:], in_=rnorm_in[:])
+
+            widen_noise("vector", 0)
+            weave_noise("vector", 0, 0)
+            weave_noise("vector", 0, 1)
+            quantize_noise(0)
+            turned = {}
+            for g in range(PASSES):
+                for a in range(2):
+                    turned[g, a] = turn_factor(g, a)
+            empty_factor(nc.scalar.copy, turned[0, 0], 0, 0)
+            empty_factor(nc.scalar.copy, turned[0, 1], 0, 1)
+            quantize_factor(0)
+            empty_factor(nc.scalar.copy, turned[1, 0], 1, 0)
+            empty_factor(nc.vector.tensor_copy, turned[1, 1], 1, 1)
+            quantize_factor(1)
+
+            basis_bank = {}
+            for g in range(PASSES):
+                w_tiles(0, g)
+                for quarter in range(4):
+                    empty_woven(first_woven(g, quarter), g, quarter)
+                if g == 0:
+                    for n in range(2):
+                        basis_bank[n] = turn_basis(n)
+            for g in range(PASSES):
+                quantize_w(0, g, whole)
+
+            widen_noise("scalar", 1)
+            weave_noise("gpsimd", 1, 0)
+            weave_noise("gpsimd", 1, 1)
+            quantize_noise(1)
+            widen_noise("scalar", 2)
+            weave_noise("gpsimd", 2, 0)
+            weave_noise("vector", 2, 1)
+
+            for n in range(TILES):
+                if n >= 2:
+                    basis_bank[n] = turn_basis(n)
+                empty_basis(basis_bank[n], n)
+                if n % 2 == 1:
+                    quantize_basis(n - 1)
+            quantize_noise(2)
+
+            issued = 0
+            for s in range(CHUNKS * TILES):
+                if s == 5:
+                    widen_noise("scalar", 3)
+                while issued < FIRST_ISSUED[min(s, len(FIRST_ISSUED) - 1)]:
+                    c, bank_of_chunk = divmod(issued, PASSES * PACK)
+                    g, t = divmod(bank_of_chunk, PACK)
+                    first_plane(c + 1, g, t)
+                    issued += 1
+
+                if s == 0:
+                    for half in range(2):
+                        weave_w("vector", 1, 0, half)
+                    for half in range(2):
+                        quantize_w(1, 0, halves[half])
+                if s == 3:
+                    weave_w("gpsimd", 1, 1, 0)
+                    weave_w("vector", 1, 1, 1)
+                    for half in range(2):
+                        quantize_w(1, 1, halves[half])
+                if s == 11:
+                    for half in range(2):
+                        weave_noise("gpsimd", 3, half)
+                    quantize_noise(3)
+                if s == 14:
+                    for engine, g in (("scalar", 1), ("gpsimd", 0)):
+                        weave_w(engine, 2, g, 1)
+                        weave_w(engine, 2, g, 0)
+                        quantize_w(2, g, whole)
+                if s == 22:
+                    for g, engines in enumerate((("gpsimd", "scalar"), ("scalar", "gpsimd"))):
+                        for half in range(2):
+                            weave_w(engines[half], 3, g, half)
+                        quantize_w(3, g, whole)
+
+                finish_tile(s, second_tile(s))

from contextlib import ExitStack

import concourse.mybir as mybir
from concourse.masks import make_identity

T, B, R, N = 1024, 1024, 512, 2048
FLOPS = 2 * B * R * N + 2 * T * B * N

F32 = mybir.dt.float32
BF16 = mybir.dt.bfloat16
U32 = mybir.dt.uint32
U8 = mybir.dt.uint8
FP8 = mybir.dt.float8_e4m3fn
FP8X4 = mybir.dt.float8_e4m3fn_x4
ADD = mybir.AluOpType.add
MULT = mybir.AluOpType.mult
COPY = mybir.ActivationFunctionType.Copy
IDENTITY = mybir.ActivationFunctionType.Identity

P = 128
PACK = 4
PASSES = B // (P * PACK)
CHUNK = 512
HALF = CHUNK // 2
CHUNKS = N // CHUNK
TILES = T // P
LAST = CHUNKS * TILES - 1

FIRST_ISSUED = (5, 6, 7, 9, 10, 11, 13, 14, 15, 16, 16, 16, 16, 16, 16, 19, 23, 24)


def tile_promp_trajectory_sampling_s7_kernel(
    tc, factor, noise_bytes, noise_scale, mean, basis, rnorm, amp, out
):
    nc = tc.nc
    with ExitStack() as ctx:
        keep = ctx.enter_context(tc.tile_pool(name="keep", bufs=1))
        stage = ctx.enter_context(tc.tile_pool(name="stage", bufs=3))
        psum_first = ctx.enter_context(tc.psum_pool(name="psum_first", bufs=4))
        psum_second = ctx.enter_context(tc.psum_pool(name="psum_second", bufs=4))

        factor_rows = keep.tile([P, PASSES, PACK, R], BF16, name="factor_rows")
        factor_woven = keep.tile([P, PASSES, PACK, P, PACK], BF16, name="factor_woven", align_bytes=64)
        factor_codes = keep.tile([P, PASSES, PACK * P], U32, name="factor_codes", align_bytes=64)
        factor_scales = keep.tile([P, PASSES, PACK * P], U8, name="factor_scales", align_bytes=64)
        basis_rows = keep.tile([P, TILES, B], BF16, name="basis_rows")
        basis_woven = keep.tile([P, TILES, PASSES, P, PACK], BF16, name="basis_woven", align_bytes=64)
        basis_codes = keep.tile([P, TILES, PASSES * P], U32, name="basis_codes", align_bytes=64)
        basis_scales = keep.tile([P, TILES, PASSES * P], U8, name="basis_scales", align_bytes=64)
        noise_codes_in = keep.tile([P, CHUNKS, PACK, CHUNK], U8, name="noise_codes_in")
        noise_codes = keep.tile([P, CHUNKS, CHUNK], U32, name="noise_codes", align_bytes=64)
        noise_scales = keep.tile([P, CHUNKS, CHUNK], U8, name="noise_scales", align_bytes=64)
        byte_scale = keep.tile([P, PACK], F32, name="byte_scale")
        mean_in = keep.tile([P, PASSES, PACK], BF16, name="mean_in")
        mean_f32 = keep.tile([P, PASSES, PACK], F32, name="mean_f32")
        rnorm_in = keep.tile([P, TILES], BF16, name="rnorm_in")
        rnorm_f32 = keep.tile([P, TILES], F32, name="rnorm_f32")
        amp_all = keep.tile([P, N], BF16, name="amp_all")
        identity = keep.tile([P, P], F32, name="identity")
        warm = keep.tile([P, 1], F32, name="warm")

        factor_hbm = factor.rearrange("(g m t) r -> g m t r", g=PASSES, t=PACK)
        noise_hbm = noise_bytes.rearrange("(p t) (c j) -> c p t j", t=PACK, j=CHUNK)
        basis_hbm = basis.rearrange("(p n) b -> p n b", n=TILES)
        out_hbm = out.rearrange("(p n) j -> p n j", n=TILES)

        def load_factor(g, a):
            slots = slice(2 * a, 2 * a + 2)
            nc.sync.dma_start(out=factor_rows[:, g, slots, :], in_=factor_hbm[g][:, slots, :])

        def load_noise(c):
            nc.sync.dma_start(out=noise_codes_in[:, c], in_=noise_hbm[c])

        def load_basis(n):
            nc.sync.dma_start(out=basis_rows[:, n : n + 2, :], in_=basis_hbm[:, n : n + 2, :])

        def load_amp(first, end):
            cols = slice(CHUNK * first, CHUNK * end)
            nc.sync.dma_start(out=amp_all[:, cols], in_=amp[cols].partition_broadcast(P))

        nc.sync.dma_start(out=byte_scale[:], in_=noise_scale.rearrange("(p t) o -> p (t o)", t=PACK))
        nc.scalar.dma_start(out=mean_in[:], in_=mean.rearrange("(g p t) -> p g t", g=PASSES, t=PACK))
        nc.scalar.dma_start(out=rnorm_in[:], in_=rnorm.rearrange("(p n) -> p n", n=TILES))
        for t in (0, 2):
            nc.sync.dma_start(out=noise_codes_in[:, 0, t : t + 2], in_=noise_hbm[0][:, t : t + 2])
        for g in range(PASSES):
            for a in range(2):
                load_factor(g, a)
        load_basis(0)
        load_noise(1)
        load_basis(2)
        load_noise(2)
        load_basis(4)
        load_amp(0, 1)
        load_basis(6)
        load_noise(3)
        load_amp(1, CHUNKS)

        make_identity(nc, identity[:])
        nc.vector.memset(warm[:], 0.0)
        nc.scalar.activation(out=warm[:], in_=warm[:], func=IDENTITY)

        factor_words = factor_rows[:].bitcast(F32)
        basis_words = basis_rows[:].bitcast(F32)

        def turn_factor(g, a):
            bank = psum_first.tile([P, 2, 2, P], F32, name="bank_first")
            for x in range(2):
                for u in range(2):
                    nc.tensor.transpose(bank[:, x, u, :], factor_words[:, g, 2 * a + x, u::2], identity[:])
            return bank

        def empty_factor(copy, bank, g, a):
            woven = factor_woven[:, g, 2 * a : 2 * a + 2].rearrange("p x m t -> p (x m t)").bitcast(F32)
            copy(
                out=woven.rearrange("p (x m u) -> p x m u", x=2, u=2),
                in_=bank[:].rearrange("p x u m -> p x m u"),
            )

        def quantize_factor(g):
            nc.vector.quantize_mx(
                out=factor_codes[:, g].bitcast(FP8X4),
                scales=factor_scales[:, g],
                in_=factor_woven[:, g].rearrange("p t m k -> p (t m k)"),
            )

        def turn_basis(n):
            bank = psum_second.tile([P, PASSES, 2, P], F32, name="bank_second")
            for g in range(PASSES):
                first = P * 2 * g
                for u in range(2):
                    words = slice(first + u, first + P * 2, 2)
                    nc.tensor.transpose(bank[:, g, u, :], basis_words[:, n, words], identity[:])
            return bank

        def empty_basis(bank, n):
            woven = basis_woven[:, n].rearrange("p g m t -> p (g m t)").bitcast(F32)
            nc.scalar.copy(
                out=woven.rearrange("p (g m u) -> p g m u", g=PASSES, u=2),
                in_=bank[:].rearrange("p g u m -> p g m u"),
            )

        def quantize_basis(n):
            pair = slice(n, n + 2)
            nc.vector.quantize_mx(
                out=basis_codes[:, pair].rearrange("p n k -> p (n k)").bitcast(FP8X4),
                scales=basis_scales[:, pair].rearrange("p n k -> p (n k)"),
                in_=basis_woven[:, pair].rearrange("p n g m t -> p (n g m t)"),
            )

        def weave(engine, woven, planes, half):
            cols = slice(HALF * half, HALF * (half + 1))
            dst = woven[:, cols, :]
            src = planes[:, :, cols]
            if engine == "gpsimd":
                nc.gpsimd.tensor_scalar(
                    out=dst, in0=src.rearrange("p t j -> p j t"), scalar1=1.0, scalar2=0.0, op0=MULT, op1=ADD
                )
                return
            copy = nc.scalar.copy if engine == "scalar" else nc.vector.tensor_copy
            copy(
                out=dst.rearrange("p (j i) t -> p j t i", i=4),
                in_=src.rearrange("p t (j i) -> p j t i", i=4),
            )

        noise_planes = {}
        noise_woven = {}

        def widen_noise(engine, c):
            noise_planes[c] = stage.tile([P, PACK, CHUNK], BF16, name="noise_planes")
            noise_woven[c] = stage.tile([P, CHUNK, PACK], BF16, name="noise_woven", align_bytes=64)
            for t in range(PACK):
                src = noise_codes_in[:, c, t, :].bitcast(FP8)
                dst = noise_planes[c][:, t, :]
                scale = byte_scale[:, t : t + 1]
                if engine == "scalar":
                    nc.scalar.activation(out=dst, in_=src, func=COPY, scale=scale)
                else:
                    nc.vector.tensor_scalar(out=dst, in0=src, scalar1=scale, scalar2=None, op0=MULT)

        def weave_noise(engine, c, half):
            weave(engine, noise_woven[c], noise_planes[c], half)

        def quantize_noise(c):
            nc.vector.quantize_mx(
                out=noise_codes[:, c].bitcast(FP8X4),
                scales=noise_scales[:, c],
                in_=noise_woven[c][:].rearrange("p j t -> p (j t)"),
            )

        w_planes = {}
        w_woven = {}
        w_codes = {}
        w_scales = {}

        def first_pass(bank, g, t, c, cols):
            rows = slice(P * t, P * (t + 1))
            nc.tensor.matmul_mx(
                out=bank,
                lhsT=factor_codes[:, g, rows].bitcast(FP8X4),
                lhsT_scale=factor_scales[:, g, rows],
                rhs=noise_codes[:, c, cols].bitcast(FP8X4),
                rhs_scale=noise_scales[:, c, cols],
                start=True,
                stop=True,
            )

        def w_tiles(c, g):
            w_woven[c, g] = stage.tile([P, CHUNK, PACK], BF16, name="w_woven", align_bytes=64, bufs=4)
            w_codes[c, g] = stage.tile([P, CHUNK], U32, name="w_codes", align_bytes=64, bufs=6)
            w_scales[c, g] = stage.tile([P, CHUNK], U8, name="w_scales", align_bytes=64, bufs=6)

        def first_woven(g, quarter):
            bank = psum_first.tile([P, PACK, P], F32, name="bank_first")
            cols = slice(P * quarter, P * (quarter + 1))
            for t in range(PACK):
                first_pass(bank[:, t, :], g, t, 0, cols)
            return bank

        def empty_woven(bank, g, quarter):
            nc.vector.tensor_tensor(
                out=w_woven[0, g][:, P * quarter : P * (quarter + 1), :],
                in0=bank[:].rearrange("p t j -> p j t"),
                in1=mean_f32[:, g, :].unsqueeze(1).to_broadcast([P, P, PACK]),
                op=ADD,
            )

        def first_plane(c, g, t):
            if t == 0:
                w_tiles(c, g)
                w_planes[c, g] = stage.tile([P, PACK, CHUNK], BF16, name="w_planes", bufs=4)
            bank = psum_first.tile([P, CHUNK], F32, name="bank_first")
            first_pass(bank[:], g, t, c, slice(0, CHUNK))
            nc.scalar.activation(
                out=w_planes[c, g][:, t, :], in_=bank[:], func=IDENTITY, bias=mean_f32[:, g, t : t + 1]
            )

        def weave_w(engine, c, g, half):
            weave(engine, w_woven[c, g], w_planes[c, g], half)

        def quantize_w(c, g, cols):
            nc.vector.quantize_mx(
                out=w_codes[c, g][:, cols].bitcast(FP8X4),
                scales=w_scales[c, g][:, cols],
                in_=w_woven[c, g][:, cols, :].rearrange("p j t -> p (j t)"),
            )

        whole = slice(0, CHUNK)
        halves = (slice(0, HALF), slice(HALF, CHUNK))

        results = {}

        def second_tile(s):
            c, n = divmod(s, TILES)
            bank = psum_second.tile([P, CHUNK], F32, name="bank_second")
            for g in range(PASSES):
                phases = slice(P * g, P * (g + 1))
                nc.tensor.matmul_mx(
                    out=bank[:],
                    lhsT=basis_codes[:, n, phases].bitcast(FP8X4),
                    lhsT_scale=basis_scales[:, n, phases],
                    rhs=w_codes[c, g][:].bitcast(FP8X4),
                    rhs_scale=w_scales[c, g][:],
                    start=(g == 0),
                    stop=(g == PASSES - 1),
                )
            return bank

        def finish_tile(s, bank):
            c, n = divmod(s, TILES)
            if n % 2 == 0:
                results[s // 2] = stage.tile([P, 2, CHUNK], F32, name="result", bufs=5)
            result = results[s // 2]
            for cols in halves if s == LAST else (whole,):
                out_cols = slice(CHUNK * c + cols.start, CHUNK * c + cols.stop)
                nc.vector.scalar_tensor_tensor(
                    out=result[:, n % 2, cols],
                    in0=bank[:, cols],
                    scalar=rnorm_f32[:, n : n + 1],
                    in1=amp_all[:, out_cols],
                    op0=MULT,
                    op1=MULT,
                )
                if s >= LAST - 1:
                    nc.sync.dma_start(out=out_hbm[:, n, out_cols], in_=result[:, n % 2, cols])
            if n % 2 == 1 and s != LAST:
                nc.sync.dma_start(out=out_hbm[:, n - 1 : n + 1, CHUNK * c : CHUNK * (c + 1)], in_=result[:])

        with tc.manual_schedule():
            nc.vector.tensor_copy(out=mean_f32[:], in_=mean_in[:])
            nc.vector.tensor_copy(out=rnorm_f32[:], in_=rnorm_in[:])

            widen_noise("vector", 0)
            weave_noise("vector", 0, 0)
            weave_noise("vector", 0, 1)
            quantize_noise(0)
            turned = {}
            for g in range(PASSES):
                for a in range(2):
                    turned[g, a] = turn_factor(g, a)
            empty_factor(nc.scalar.copy, turned[0, 0], 0, 0)
            empty_factor(nc.scalar.copy, turned[0, 1], 0, 1)
            quantize_factor(0)
            empty_factor(nc.scalar.copy, turned[1, 0], 1, 0)
            empty_factor(nc.vector.tensor_copy, turned[1, 1], 1, 1)
            quantize_factor(1)

            basis_bank = {}
            for g in range(PASSES):
                w_tiles(0, g)
                for quarter in range(4):
                    empty_woven(first_woven(g, quarter), g, quarter)
                if g == 0:
                    for n in range(2):
                        basis_bank[n] = turn_basis(n)
            for g in range(PASSES):
                quantize_w(0, g, whole)

            widen_noise("scalar", 1)
            weave_noise("gpsimd", 1, 0)
            weave_noise("gpsimd", 1, 1)
            quantize_noise(1)
            widen_noise("scalar", 2)
            weave_noise("gpsimd", 2, 0)
            weave_noise("vector", 2, 1)

            for n in range(TILES):
                if n >= 2:
                    basis_bank[n] = turn_basis(n)
                empty_basis(basis_bank[n], n)
                if n % 2 == 1:
                    quantize_basis(n - 1)
            quantize_noise(2)

            issued = 0
            for s in range(CHUNKS * TILES):
                if s == 5:
                    widen_noise("scalar", 3)
                while issued < FIRST_ISSUED[min(s, len(FIRST_ISSUED) - 1)]:
                    c, bank_of_chunk = divmod(issued, PASSES * PACK)
                    g, t = divmod(bank_of_chunk, PACK)
                    first_plane(c + 1, g, t)
                    issued += 1

                if s == 0:
                    for half in range(2):
                        weave_w("vector", 1, 0, half)
                    for half in range(2):
                        quantize_w(1, 0, halves[half])
                if s == 3:
                    weave_w("gpsimd", 1, 1, 0)
                    weave_w("vector", 1, 1, 1)
                    for half in range(2):
                        quantize_w(1, 1, halves[half])
                if s == 11:
                    for half in range(2):
                        weave_noise("gpsimd", 3, half)
                    quantize_noise(3)
                if s == 14:
                    for engine, g in (("scalar", 1), ("gpsimd", 0)):
                        weave_w(engine, 2, g, 1)
                        weave_w(engine, 2, g, 0)
                        quantize_w(2, g, whole)
                if s == 22:
                    for g, engines in enumerate((("gpsimd", "scalar"), ("scalar", "gpsimd"))):
                        for half in range(2):
                            weave_w(engines[half], 3, g, half)
                        quantize_w(3, g, whole)

                finish_tile(s, second_tile(s))
